import numpy as np, ml_dtypes
CORES = [23,119,17,113]
N = 4
BF = ml_dtypes.bfloat16
def gentries(a):
    return np.ascontiguousarray(a.reshape(8, 16, -1).transpose(0, 2, 1)).reshape(8, -1)
def gtable(e):
    e = np.asarray(e); return np.ascontiguousarray(e.reshape(8, -1, 16).transpose(0, 2, 1)).reshape(128, -1).astype(np.int32)
V, RO, SH = 1024, 2, 1
W = N * V
E = 16 * W
def join(ro, a, b):
    ro[a] = b; ro[b] = a
def couple(rng, ro, q):
    q = rng.permutation(q); h = len(q) // 2
    join(ro, q[:h], q[h:2 * h])
    if len(q) > 2 * h: ro[q[-1]] = q[-1]
def rest(rng, ro):
    couple(rng, ro, np.flatnonzero(ro < 0))
def pack(ro, X):
    x = np.ascontiguousarray(X.reshape(8, N, V, 16).transpose(1, 0, 3, 2)).reshape(N, 128, V)
    return {"rot": np.stack([gtable(ro[:, 16 * V * r:16 * V * (r + 1)]) for r in range(N)]), "x": x.astype(np.float32).astype(BF)}
def parities(rng, mode):
    par = np.zeros((8, N, V), np.int64)
    for r in range(N):
        c = int(mode[r])
        if c == 4: par[:, r] = rng.integers(0, 2, (8, V))
        if c in (1, 2): par[:, r] = 1
        if c in (2, 3): par[int(rng.integers(0, 8)), r, int(rng.integers(0, V))] ^= 1
    return par.reshape(8, W)
def voted(rng, ro, h, par, one):
    s = np.argsort(rng.random((W, 8)), axis=1)[:, :2]
    if one: s = np.full((W, 1), int(rng.integers(0, 8)))
    c = np.zeros((W, 16), bool); np.put_along_axis(c, 2 * s + par[:, None], True, 1); c = c.reshape(-1)
    free = ro < 0; hh = np.repeat(h, 16)
    join(ro, rng.permutation(np.flatnonzero(free & c & hh)), rng.permutation(np.flatnonzero(free & c & ~hh)))
    couple(rng, ro, np.flatnonzero(free & ~c & hh)); couple(rng, ro, np.flatnonzero(free & ~c & ~hh))
def nearly(rng, ro, X):
    q = np.concatenate([np.array([W - 1, 0]), 1 + rng.permutation(W - 2)[:10]])
    for b in range(4):
        i, j = sorted(int(v) for v in rng.permutation(16)[:2])
        if b & 1: i, j = j, i
        w, u, z = int(q[b]), int(q[4 + 2 * b]), int(q[5 + 2 * b]); e = 255 * int(rng.integers(0, 2))
        X[w] = e; X[u] = 255 - e; X[z] = 255 - e; X[u, int(rng.integers(0, 16))] = abs(254 - e)
        join(ro, 16 * w + i, 16 * u + int(rng.integers(0, 16))); join(ro, 16 * w + j, 16 * z + int(rng.integers(0, 16)))
def setup_inputs(rng):
    ro = np.full((8, E), -1, np.int64); X = rng.integers(0, 256, (8, W, 16))
    s = rng.integers(0, 32, (8, 8, 16)); pal = np.where(rng.random(s.shape) < 0.5, s, 255 - s)
    X = np.where(rng.random((8, W, 1)) < 0.25, pal[np.arange(8)[:, None], rng.integers(0, 8, (8, W))], X)
    for g in range(8):
        q = rng.permutation(E)[:32]; ro[g, q] = q
        rest(rng, ro[g])
    return pack(ro, X)
def setup_inputs_spread(rng):
    ro = np.full((8, E), -1, np.int64)
    X = np.minimum((np.exp2(9 * rng.random((8, W, 1)) - 2 * rng.random((8, 1, 16))) * rng.random((8, W, 16))).astype(np.int64), 255)
    share = rng.permutation(np.array([0.0, 0.1, 0.3, 0.5, 0.7, 0.8, 0.9, 0.97])); q = rng.permutation(N)
    for g in range(8):
        join(ro[g], 16 * V * int(q[0]) + rng.permutation(16 * V), 16 * V * int(q[1]) + rng.permutation(16 * V))
        for r in q[2:]:
            couple(rng, ro[g], 16 * V * int(r) + np.flatnonzero(rng.random(16 * V) < share[g]))
        rest(rng, ro[g])
    return pack(ro, X)
def setup_inputs_ends(rng):
    ro = np.full((8, E), -1, np.int64); mode = np.full(N, 4); mode[:3] = (0, 2, 3); mode[N - 1] = 1
    par = parities(rng, mode); X = np.zeros((8, W, 16), np.int64); z = 16 * (W - 1)
    for g in range(8):
        h = np.zeros(W, bool); h[rng.permutation(np.arange(1, W - 1))[:W // 2 - 1]] = True; h[W - 1] = True
        for i, j in (((15, 0), (1, 14), (8, 3)) if g % 2 == 1 else ((15, 0),)): join(ro[g], z + i, j)
        couple(rng, ro[g], z + np.flatnonzero(ro[g, z:] < 0)); couple(rng, ro[g], np.flatnonzero(ro[g, :16] < 0))
        voted(rng, ro[g], h, par[g], False)
        flip = np.zeros((W, 16), bool); np.put_along_axis(flip, rng.integers(0, 16, (W, 2)), True, 1)
        flip &= rng.random((W, 1)) < 0.75; flip[0] = False; flip[W - 1] = False
        X[g] = np.where(h[:, None] ^ flip, 255, 0)
    return pack(ro, X)
def setup_inputs_crowd(rng):
    ro = np.full((8, E), -1, np.int64); par = parities(rng, rng.permutation(N) & 3); X = np.zeros((8, W, 16), np.int64)
    for g in range(8):
        h = rng.permutation(W) < W // 2
        voted(rng, ro[g], h, par[g], g % 4 == 0)
        X[g] = rng.integers(0, 64, (W, 16)) + 192 * h[:, None]
    return pack(ro, X)
def setup_inputs_corners(rng):
    ro = np.full((8, E), -1, np.int64); a = np.arange(E); w = np.arange(W); kind = rng.permutation(8)
    for g in range(8):
        c = int(kind[g]); s = int(rng.integers(1, 16))
        if c == 0: ro[g] = a
        elif c == 1: ro[g] = a ^ s
        elif c == 2: ro[g] = E - 1 - a
        elif c == 3:
            for r in range(N): couple(rng, ro[g], 16 * V * r + np.arange(16 * V))
        elif c == 4: ro[g] = ((a + E // 2) % E) ^ s
        elif c == 5:
            step = (1, 2, 3, V, V - 1, W // 2, W - 1, 0)
            for b in range(8): join(ro[g], 16 * w + 2 * b, 16 * ((w + step[b]) % W) + 2 * b + 1)
        elif c == 6:
            q = rng.permutation(E)[:E // 2]; ro[g, q] = q; rest(rng, ro[g])
        else:
            join(ro[g], np.arange(16), E - 1 - np.arange(16)); rest(rng, ro[g])
    X = rng.integers(0, 256, (8, W, 16)); at = np.argsort(kind); o = at[rng.permutation(np.array([0, 1, 2, 4, 5]))]
    X[at[6]] = rng.integers(0, 256, 16)
    X[at[3]] = rng.integers(0, 255, 16) + rng.integers(0, 2, (W, 1))
    X[at[7]] = 255 * rng.integers(0, 2, (W, 1))
    X[o[0]] = 0; X[o[0], W - 1] = 255
    X[o[1]] = rng.integers(0, 2, (W, 16)); X[o[2]] = 255 - rng.integers(0, 3, (W, 16))
    return pack(ro, X)
def setup_inputs_ties(rng):
    ro = np.full((8, E), -1, np.int64); X = np.zeros((8, W, 16), np.int64)
    for g in range(8):
        b = rng.integers(64, 192, 16); d = rng.integers(1, 61, 16)
        X[g] = np.stack([b, b + d, b - d, b + rng.permutation(d)])[rng.integers(0, 4, W)]
        nearly(rng, ro[g], X[g])
        rest(rng, ro[g])
    return pack(ro, X)
def check_inputs(d):
    bad = []
    xf = np.asarray(d["x"]).astype(np.float64); r = np.asarray(d["rot"]).astype(np.int64)
    if not (np.min(xf) >= 0 and np.max(xf) <= 255): bad.append("range of x")
    if not np.array_equal(xf, np.floor(xf)): bad.append("whole numbers of x")
    if np.min(r) < 0 or np.max(r) > E - 1: bad.append("range of rot")
    full = np.clip(np.concatenate([gentries(a) for a in r], axis=1), 0, E - 1)
    if not np.array_equal(np.take_along_axis(full, full, 1), np.tile(np.arange(E), (8, 1))): bad.append("rot is its own inverse")
    return bad
def reference(rot, x):
    R = np.concatenate([gentries(a) for a in rot], axis=1).astype(np.int64)
    X = np.ascontiguousarray(x.astype(np.float32).astype(np.int32).reshape(N, 8, 16, V).transpose(1, 0, 3, 2)).reshape(8, W, 16)
    g = np.arange(8)[:, None]
    for t in range(RO):
        far = R >> 4
        Y = X[g, far].reshape(8, W, 16, 16)
        score = np.add.reduce(np.abs(Y - X[:, :, None, :]), axis=3)
        k = np.argmax(score, axis=2)
        A = np.add.reduce((k & 1).reshape(8, N, V), axis=(0, 2))
        m = (k + np.repeat(A, V)[None, :]) & 15; m = np.where(m == 0, 15, m)
        S = np.take_along_axis(R, 16 * far + ((R & 15) ^ m[g, far]), 1)
        X = ((2 ** SH - 1) * X + np.take_along_axis(Y, k[:, :, None, None], 2)[:, :, 0]) >> SH
        R = S
    yr = R.reshape(8, N, V, 16).transpose(1, 0, 3, 2).reshape(N, 128, V)
    yx = X.reshape(8, N, V, 16).transpose(1, 0, 3, 2).reshape(N, 128, V)
    return {"yr": np.ascontiguousarray(yr).astype(np.float32), "yx": np.ascontiguousarray(yx).astype(np.float32).astype(BF)}

@@ -1,0 +1,721 @@
+from concourse.bass import DstId, RemoteDMATransfer, IndirectOffsetOnAxis
+from concourse.mybir import AluOpType as OP, AxisListType, ActivationFunctionType as AF
+
+BF, F32, I32, U16 = "bfloat16", "float32", "int32", "uint16"
+
+
+def _sb(n, d):
+    return ("sbuf", [128, n], d)
+
+
+SCRATCH = {
+    "ps": ("psum", [128, 4096], F32),
+    "XT0": _sb(4096, BF), "XT1": _sb(4096, BF), "RT0": _sb(8192, BF), "RT1": _sb(8192, BF),
+    "DY": _sb(16384, BF), "VER": _sb(16384, BF), "AB": _sb(6144, BF), "BP": _sb(9216, BF),
+    "rot_i": _sb(1024, I32),
+    "N2": _sb(2048, BF), "T2": _sb(2048, BF), "W2": _sb(2048, F32), "sm": _sb(1024, F32),
+    "o4": _sb(1024, U16), "o3": _sb(1024, U16), "o3b": _sb(1024, U16),
+    "jb": _sb(1024, BF), "tA": _sb(2048, BF), "n2N": _sb(1024, BF), "n2W": _sb(1024, BF), "jw": _sb(1024, BF),
+    "Zh": _sb(1024, BF), "X2": _sb(1024, BF), "XO": _sb(1024, BF),
+    "kf": _sb(512, F32), "sf": _sb(1024, F32), "si": _sb(512, I32), "sb": _sb(64, BF), "su": _sb(256, U16),
+    "ci": _sb(64, I32), "cf": _sb(64, F32), "XI": _sb(144, F32), "XH": _sb(128, F32), "XG": _sb(128, F32),
+    "VL": _sb(128, F32), "tm": _sb(384, F32), "Wv": _sb(192, F32), "I32m": _sb(128, F32), "CI": _sb(16, F32),
+    "M": _sb(20 * 128, BF), "WB": _sb(2048, BF), "Zw": _sb(144, BF), "Z2": _sb(144, BF), "Wg": _sb(32, BF),
+    "CT": _sb(1024, BF), "PI": _sb(16, I32),
+    "LD": ("dram", [128, 2048], BF),
+}
+NDMA = 56
+WINDOW, SLOPE, GATHER = 0.0, 0.0, 1.5
+KEEP = ("g", "s", "v", "a")
+PIECES = 4
+SEMAPHORES = (["cv", "ca", "ct", "cg"] + ["d%d" % k for k in range(NDMA)]
+              + ["ax1"] + ["%s%d%d" % (s, t, h) for s in ("ap", "as", "af") for t in range(3) for h in range(4)])
+(mI, mNI, m256, m64k, mPig, mWc, mL00, mL01, mL10, mL11, mC0, mC1, mT0, mT1, mDF, mOne, mGV0, mGV1, mWl, m8) = range(20)
+R256 = 1.5 * 2.0 ** 31
+R1 = 1.5 * 2.0 ** 23
+EIGHTH = 192 - 0.4375
+
+VOTE1 = ("A0 D3 A1 S0 S1 R3 D4 P0 S2 P1 S3 T0 A2 D5 R5 P2 S4 P3 S5 T1 D6 Q4 x0 D7 P4 P5 T2 j1 Q6 j3 R7 x1")
+MIDDLE = ("b3 b4 c0 c2 a3 a4 g0 l0 a5 m3 b5 l3 g1 w0 l1 a6 m4 b6 l4 a7 m5 b7 w2 g2 w1 a14 m6 b14 a15 m7 w3 b15 l5 l2 l6 l7 "
+          "a13 g8 o0 A0 L0 m14 b13 g9 w4 A1 m15 w7 m13 c1 l8 l9 S0 S1 l14 l15 l13 g10 l10 g11 w5 P0 P1 l11 S2 A2 g12 l12 w6 "
+          "L1 S3 T0 D3 P2 S4 P3 S5 T1 o1 R3 P4 P5 T2 A7 D4 S14 S15 x0 D5 Q4 P14 P15 T7 D6 Q5 j0 j2 j3 R6 x1")
+LAST = ("c3 a3 b3 a4 b4 g0 a5 m3 b5 g1 a6 m4 b6 a7 m5 b7 g2 a10 m6 b10 a11 m7 b11 g8 a12 m10 b12 a13 m11 b13 g9 "
+        "a14 m12 b14 a15 m13 b15 m14 m15")
+
+
+def rank_program(g, core, T, topo):
+    rank = T.rank_of(core)
+    if rank is None:
+        return
+    others = [c for c in T.cores if c != core]
+    sib = [c for c in others if topo.chip(c) == topo.chip(core)][0]
+    peer = [c for c in others if topo.chip(c) != topo.chip(core) and topo.die(c) == topo.die(core)][0]
+    diag = [c for c in others if c != sib and c != peer][0]
+    Q = {"v": g.vector, "a": g.scalar, "t": g.tensor, "g": g, "s": g.sync}
+    ops = []
+    ndma = [0]
+
+    def A(name, lo, hi, step=1, p=None, reg=None):
+        t = T[name]
+        ps = slice(0, 128) if p is None else slice(p[0], p[1])
+        ap = t[ps, lo:hi] if step == 1 else t[ps, lo:hi:step]
+        return (ap, (name,) + (reg if reg else (lo, hi)) + (-(-(hi - lo) // step),))
+
+    def B(name, k, n):
+        return A(name, n * k, n * k + n)
+
+    def Mx(k, n=128):
+        return A("M", 128 * k, 128 * k + n)
+
+    def col(name, j):
+        return A(name, j, j + 1)
+
+    def G(win, off):
+        return (win[0].indirect(off[0]), win[1], off[1])
+
+    def regs(xs):
+        out = []
+        for x in xs:
+            if isinstance(x, tuple):
+                out.extend(r[:3] for r in x[1:])
+        return out
+
+    def val(x):
+        return x[0] if isinstance(x, tuple) else x
+
+    def short(*xs):
+        return 0.5 if all(SCRATCH[x[1][0]][2] in (BF, U16) for x in xs) else 1.0
+
+    def add(q, fn, rd, wr, kind="c", sem=None, n=1, rate=1.0):
+        if kind in ("d", "r"):
+            sem = "d%d" % ndma[0]
+            ndma[0] += 1
+        size = lambda x: x[1][3]
+        lat = 90
+        if kind == "x":
+            cost, lat = 0, {"p": 6000, "s": 4500, "f": 4000, "x": 11000}[sem[1]]
+        elif kind == "r":
+            cost, lat = 700, 3000
+        elif kind == "d":
+            cost, lat = (1700 if q == "g" else 60), 3500
+        elif q == "t":
+            cost, lat = max(64, size(rd[1])) * (2.0 if rd[0][1][0] == "kf" else 0.5), 190
+        elif q == "g":
+            cost = 130 + 2 * size(wr[0])
+        elif rd and len(rd[0]) == 3:
+            cost = 60 + GATHER * 16 * (rd[0][2][2] - rd[0][2][1])
+        else:
+            cost = 60 + max(40, size(wr[0]) * rate)
+        ops.append({"q": q, "fn": fn, "rd": regs(rd), "wr": regs(wr), "kind": kind, "sem": sem, "n": n, "cost": cost, "lat": lat})
+
+    def ts(out, in0, s1, o0, s2=None, o1=None):
+        if o1 is None:
+            add("v", lambda: g.vector.tensor_scalar(out[0], in0[0], val(s1), None, o0), [in0, s1], [out], rate=short(out, in0))
+        else:
+            add("v", lambda: g.vector.tensor_scalar(out[0], in0[0], val(s1), val(s2), o0, o1), [in0, s1, s2], [out],
+                rate=short(out, in0))
+
+    def tt(out, a, b, op):
+        add("v", lambda: g.vector.tensor_tensor(out[0], a[0], b[0], op), [a, b], [out],
+            rate=1.0 if "ps" in (a[1][0], b[1][0]) else 2.0)
+
+    def cp(out, a):
+        add("v", lambda: g.vector.tensor_copy(out[0], a[0]), [a], [out])
+
+    def act(out, a, f=AF.Copy, bias=0.0, scale=1.0):
+        add("a", lambda: g.scalar.activation(out[0], a[0], f, bias=val(bias), scale=val(scale)), [a, bias, scale], [out])
+
+    def ev(q, out, a):
+        if q == "a":
+            act(out, a)
+        else:
+            cp(out, a)
+
+    def mm(out, l, r, start, stop):
+        add("t", lambda: g.tensor.matmul(out[0], l[0], r[0], start, stop), [l, r], [out])
+
+    def iota(out, pat, base, cm, small=True):
+        if small:
+            add("g", lambda: g.iota(out[0], pat, base, cm, allow_small_or_imprecise_dtypes=True), [], [out])
+        else:
+            add("g", lambda: g.iota(out[0], pat, base, cm), [], [out])
+
+    def dma(q, out, a):
+        add(q, lambda: Q[q].dma_start(out[0], a[0]), [a], [out], kind="d", n=16)
+
+    def nbits(m):
+        return bin(m).count("1")
+
+    def send(parts):
+        def fn(ls):
+            trs = []
+            for v, dst, m, s in parts:
+                rid, pid, _ = topo.addr(dst)
+                trs.append(RemoteDMATransfer(dst_ids=[DstId(rid=rid, pnc=pid)], dma_engine_mask=m,
+                                             remote_sem=T.sem[s], src=v[0], dst=v[0]))
+            g.remote_dma_fused(trs, local_sem=ls)
+        add("g", fn, [v for v, _, _, _ in parts], [], kind="r", n=sum(nbits(m) for _, _, m, _ in parts))
+
+    def arrives(views, sem, n):
+        add(None, None, [], views, kind="x", sem=sem, n=n)
+
+    def split(src):
+        far = [c for c in T.cores if topo.chip(c) != topo.chip(src)][0]
+        near = [c for c in T.cores if c != src and topo.chip(c) == topo.chip(src)][0]
+        off = topo.mask(src, far)
+        return off, topo.mask(src, near) & ~off
+
+    def halves(src):
+        far = [c for c in T.cores if topo.chip(c) != topo.chip(src)][0]
+        e = topo.engines(src, far)
+        return sum(1 << k for k in e[:len(e) // 2]), sum(1 << k for k in e[len(e) // 2:])
+
+    def share_x(name, sem):
+        mine = B(name, rank, 1024)
+        h0, h1 = halves(core)
+        send([(mine, peer, h0, sem), (mine, diag, h1, sem), (mine, sib, split(core)[1], sem)])
+        arrives([B(name, T.rank_of(c), 1024) for c in others], sem,
+                nbits(halves(peer)[0]) + nbits(halves(diag)[1]) + nbits(split(sib)[1]))
+
+    def out_piece(name, n, k, t, h):
+        v = B(name, k * rank + h, n // k)
+        off, on = split(core)
+        send([(v, peer, off, "ap%d%d" % (t, h)), (v, sib, on, "as%d%d" % (t, h))])
+
+    def hand_on(name, n, k, t):
+        for h in range(k):
+            piece = lambda c: B(name, k * T.rank_of(c) + h, n // k)
+            arrives([piece(peer)], "ap%d%d" % (t, h), nbits(split(peer)[0]))
+            arrives([piece(sib)], "as%d%d" % (t, h), nbits(split(sib)[1]))
+            send([(piece(peer), sib, topo.mask(core, sib), "af%d%d" % (t, h))])
+            arrives([piece(diag)], "af%d%d" % (t, h), nbits(topo.mask(sib, core)))
+
+    PS = lambda lo, hi, step=1, reg=None: A("ps", lo, hi, step, None, reg)
+    hbm = lambda t, lo, hi: (t[:, lo:hi], (t.name + "_h", lo, hi))
+
+    dma("s", B("XT0", 2 * rank, 512), hbm(T.x, 0, 512))
+    dma("a", B("XT0", 2 * rank + 1, 512), hbm(T.x, 512, 1024))
+    dma("s", A("rot_i", 0, 512), hbm(T.rot, 0, 512))
+    dma("a", A("rot_i", 512, 1024), hbm(T.rot, 512, 1024))
+    dma("s", A("XO", 0, 1024), hbm(T.x, 0, 1024))
+    iota(A("ci", 0, 1), [[0, 1]], 0, 1, False)
+    iota(A("XI", 0, 144), [[1, 144]], 0, 0)
+    iota(A("XG", 0, 128), [[1, 8], [0, 16]], 0, 0)
+    iota(A("VL", 0, 128), [[0, 8], [-512, 8], [0, 2]], 256, 0)
+    out_piece("XT0", 1024, 2, 2, 0)
+    out_piece("XT0", 1024, 2, 2, 1)
+    iota(A("Wv", 0, 64), [[16, 64]], 0, 1)
+    iota(A("CT", 0, 1024, p=(0, 32)), [[-2, 8], [-1, 2], [0, 64]], 15, 0)
+    iota(A("XH", 0, 128), [[1, 64], [0, 2]], 0, 0)
+    hand_on("XT0", 1024, 2, 2)
+    p = col("ci", 0)
+    ci = lambda j: col("ci", j)
+    cf = lambda j: col("cf", j)
+    AND, SHR, EQ = OP.bitwise_and, OP.logical_shift_right, OP.is_equal
+    XI = lambda n: A("XI", 0, n)
+    ts(ci(1), p, 15, AND)
+    ts(ci(2), p, 4, SHR)
+    ts(ci(3), p, 63, AND)
+    ts(ci(4), p, 7, AND)
+    ts(ci(5), p, 3, SHR, 1, AND)
+    ts(ci(6), p, 1, AND)
+    ts(ci(7), p, 1, SHR, 7, AND)
+    for u in range(1, 8):
+        ts(ci(8 + u), p, 2 * u, AND)
+    cp(A("cf", 0, 8), A("ci", 0, 8))
+    ts(cf(8), cf(1), 8.0, OP.mult, cf(2), OP.add)
+    ts(cf(9), cf(2), 8.0, OP.mult, cf(4), OP.add)
+    ts(cf(11), cf(5), -1.0, OP.mult, 1.0, OP.add)
+    ts(cf(23), cf(1), 8.0, EQ)
+    ts(cf(24), cf(1), 0.0, EQ)
+    ts(Mx(mI), XI(128), cf(0), EQ)
+    ts(Mx(mWc, 64), XI(64), cf(3), EQ)
+    ts(Mx(mPig), XI(128), cf(8), EQ)
+    ts(A("cf", 25, 27), A("cf", 23, 25), -512.0, OP.mult, 512.0, OP.add)
+    ts(A("CI", 0, 8), XI(8), cf(1), EQ, cf(23), OP.add)
+    ts(A("CI", 8, 16), A("XI", 8, 16), cf(1), EQ, cf(24), OP.add)
+    ts(A("tm", 256, 384), A("XG", 0, 128), cf(2), EQ)
+    for h in range(2):
+        ts(B("tm", h, 128), A("VL", 0, 128), cf(23 + h), OP.mult, cf(25 + h), OP.add)
+    for h in range(2):
+        tt(Mx(mGV0 + h), B("tm", h, 128), A("tm", 256, 384), OP.mult)
+    act(Mx(mNI), Mx(mI), scale=-1.0)
+    act(A("I32m", 0, 128), Mx(mI))
+    act(Mx(m256), Mx(mI), scale=256.0)
+    act(Mx(m8), Mx(mI), scale=-8.0)
+    act(Mx(m64k), Mx(mI), scale=65536.0)
+    act(A("W2", 0, 1024), A("XO", 0, 1024), AF.Identity, bias=-0.25)
+    act(A("W2", 1024, 2048), A("XO", 0, 1024), AF.Identity, bias=-0.25, scale=0.5)
+    for h in range(2):
+        ts(B("N2", h, 512), B("rot_i", h, 512), R256, OP.add, R256, OP.subtract)
+    for h in range(2):
+        tt(B("N2", 2 + h, 512), B("rot_i", h, 512), B("N2", h, 512), OP.subtract)
+    for i in range(16):
+        act(B("WB", i, 128), Mx(mGV0 + i // 8), scale=col("CI", i))
+    ts(cf(10), cf(9), 2.0, OP.mult)
+    ts(cf(12), cf(9), 2.0, OP.mult, 1.0, OP.add)
+    ts(cf(13), cf(11), 1.0 / 256, OP.mult)
+    ts(cf(14), cf(5), 1.0 / 256, OP.mult)
+    ts(Mx(mL00), XI(128), cf(10), EQ, cf(11), OP.mult)
+    ts(Mx(mL01), XI(128), cf(12), EQ, cf(13), OP.mult)
+    ts(Mx(mL10), XI(128), cf(10), EQ, cf(5), OP.mult)
+    ts(Mx(mL11), XI(128), cf(12), EQ, cf(14), OP.mult)
+    ts(cf(15), cf(2), 16.0, OP.mult, 15.0, OP.add)
+    ts(cf(21), cf(0), 2.0, OP.add)
+    ts(cf(22), cf(1), 14.0, OP.is_lt)
+    act(cf(29), cf(11), AF.Identity, bias=1.0, scale=1535.0)
+    act(cf(30), cf(5), AF.Identity, bias=1.0, scale=1535.0)
+    for b in range(16):
+        mm(PS(128 * b, 128 * b + 128), A("N2", b, 2048, 16, reg=(0, 2048)), Mx(mPig), True, True)
+    for bank in (0, 1, 2, 3):
+        for b in range(4 * bank, 4 * bank + 4):
+            ev("av"[bank & 1], A("T2", b, 2048, 16, reg=(128 * b, 128 * b + 128)), PS(128 * b, 128 * b + 128))
+    for i in range(16):
+        mm(PS(2048 + 64 * i, 2112 + 64 * i), A("T2", 128 * i, 128 * i + 128, reg=(0, 2048)), Mx(mWc, 64), True, True)
+    for ch in range(2):
+        for h in range(2):
+            o = B("ps", 2 * ch + h, 512)
+            mm(o, Mx(mL00 + 2 * ch), B("N2", 2 + h, 512), True, False)
+            mm(o, Mx(mL01 + 2 * ch), B("N2", h, 512), False, True)
+    ts(A("tm", 1, 8), A("ci", 9, 16), -2.0, OP.mult, cf(0), OP.add)
+    ts(A("tm", 8, 16), XI(8), 2.0, OP.mult)
+    for k, w in enumerate((32.0, -16.0, 16.0)):
+        ts(B("Wg", k, 8), XI(8), cf(2), EQ, w, OP.mult)
+    tt(A("PI", 1, 8), A("tm", 1, 8), A("tm", 9, 16), OP.add)
+    add("v", lambda: g.vector.memset(Mx(mOne)[0], 1.0), [], [Mx(mOne)])
+    ts(A("Wv", 0, 64), A("Wv", 0, 64), cf(15), OP.subtract, 15.0, OP.add)
+    ts(Mx(mWl), XI(128), cf(21), EQ, cf(22), OP.mult)
+    act(A("jb", 0, 1024), A("N2", 1024, 2048), AF.Identity, bias=EIGHTH, scale=0.125)
+    for h in range(2):
+        ts(B("o4", h, 512), B("ps", 4 + h, 512), -7.5, OP.add, 1.0 / 16, OP.mult)
+    for ch in range(2):
+        act(B("VER", ch, 1024), B("ps", ch, 1024))
+    ts(A("o3", 0, 1024), PS(2048, 3072), -3.5, OP.add, 0.125, OP.mult)
+    tt(Mx(mDF), Mx(mI), Mx(mWl), OP.subtract)
+    act(A("Wv", 64, 128), A("Wv", 0, 64), AF.Identity, bias=15360.0)
+    act(A("Wv", 128, 192), A("Wv", 0, 64), AF.Identity, bias=14336.0)
+
+    def versions(hs):
+        for h in hs:
+            dma("s", (T.LD[:, 1024 * h:1024 * h + 1024], ("LD", 1024 * h, 1024 * h + 1024)), B("VER", h, 1024))
+        if 1 in hs:
+            for u in range(1, 8):
+                o = B("VER", u, 2048)
+                add("g", lambda o=o, u=u: g.indirect_dma_start(o[0], None, T.LD[:], IndirectOffsetOnAxis(ap=col("PI", u)[0], axis=0),
+                                                               bounds_check=127),
+                    [col("PI", u), (None, ("LD", 0, 2048))], [o], kind="d", n=16)
+
+    versions([0, 1])
+
+    def consts2():
+        ts(cf(31), cf(0), -64.0, OP.add)
+        ts(Mx(mWl, 64), XI(64), cf(31), EQ)
+        ts(cf(16), cf(6), 255.0, OP.mult, 1.0, OP.add)
+        ts(cf(18), cf(6), -1.0, OP.mult, 1.0, OP.add)
+        ts(cf(27), cf(11), 256.0, OP.mult)
+        ts(cf(28), cf(5), 256.0, OP.mult)
+        ts(cf(17), cf(15), -1.0, OP.add, cf(6), OP.add)
+        ts(cf(19), cf(15), -15.0, OP.add, cf(7), OP.add)
+        ts(cf(20), cf(15), -7.0, OP.add, cf(7), OP.add)
+        ts(A("Zw", 0, 144), XI(144), cf(15), EQ, cf(16), OP.mult)
+        ts(A("Z2", 0, 144), XI(144), cf(17), EQ)
+        ts(Mx(mC0), A("XH", 0, 128), cf(9), EQ, cf(27), OP.mult)
+        ts(Mx(mC1), A("XH", 0, 128), cf(9), EQ, cf(28), OP.mult)
+        ts(Mx(mT0), XI(128), cf(19), EQ, cf(18), OP.mult)
+        ts(Mx(mT1), XI(128), cf(20), EQ, cf(18), OP.mult)
+
+    slot = [3072, 3200, 3328, 3456, 3584, 3712, 2048, 2560]
+    st = {"tile": 0, "ab": 0, "nb": 1, "ag": 0}
+    abslot, gslot, bnd, pre, fin = {}, {}, {}, {}, []
+
+    def ab(ip):
+        if ip not in abslot:
+            abslot[ip] = st["ab"] % 3
+            st["ab"] += 1
+        return abslot[ip]
+
+    def red(ip, two):
+        c = slot[st["tile"]]
+        st["tile"] += 1
+        s = ab(ip)
+        mm(PS(c, c + 128), A("CT", 128 * ip, 128 * ip + 128, p=(0, 1)), A("M", 128 * mOne, 128 * mOne + 128, p=(0, 1)), True, False)
+        for name, c0, w in ([("DY", 2048 * ip, 1), ("AB", 2048 * s, 0)] if two else [("AB", 2048 * s, 2)]):
+            for b in range(16):
+                mm(PS(c + b, c + 128, 16, reg=(c, c + 128)), A(name, c0 + b, c0 + 2048, 16, reg=(c0, c0 + 2048)),
+                   B("Wg", w, 8), False, name == "AB" and b == 15)
+
+    def bound(i, c=None):
+        if c is None:
+            c = st["nb"] & 1
+            st["nb"] += 1
+        for h in range(2):
+            mm(B("ps", 2 * c + h, 512), B("WB", i, 128), B("tA", 2 * (i // 8) + h, 512), True, True)
+        return B("ps", c, 1024)
+
+    def premade(i, q, c):
+        pre[i] = B("BP", len(pre), 1024)
+        ev(q, pre[i], bound(i, c))
+
+    def done1(i):
+        pass
+
+    def wrapped(ip):
+        fin.append(("w", ip // 4))
+        for b in range(16):
+            mm(PS(3072 + 128 * ip, 3200 + 128 * ip), A("Zw", 15 - b, 143 - b),
+               A("DY", 2048 * ip + b, 2048 * ip + 2048, 16, reg=(2048 * ip, 2048 * ip + 2048)), False,
+               fin.count(("w", ip // 4)) == 4 and b == 15)
+
+    def digits(i):
+        fin.append(("l", i // 8))
+        for h in range(2):
+            mm(B("ps", 4 + h, 512), A("Z2", 14 - 2 * (i & 7), 142 - 2 * (i & 7)), B("DY", 2 * i + h, 512), False,
+               fin.count(("l", i // 8)) == 8)
+
+    def first(i):
+        if i < 2:
+            for h in range(2):
+                mm(B("ps", 4 + h, 512), Mx(mC0 + i), B("n2N", h, 512), True, False)
+        else:
+            for h in range(2):
+                o, r = (B("ps", 6 + h, 512), B("n2W", h, 512)) if i == 2 else (B("ps", 4 + h, 512), B("n2N", h, 512))
+                mm(o, Mx(m256), r, True, False)
+                mm(o, Mx(m64k), r, False, False)
+
+    def done2(i):
+        for h in range(2):
+            mm(B("ps", 4 + h, 512), A("Zw", 15 - i, 143 - i), B("DY", 2 * i + h, 512), False, len(fin) == 15)
+        fin.append(i)
+
+    def steps(text, xt, rt, off, done):
+        xw = A(xt, 0, 4096) if xt else None
+        rw = A(rt, 0, 8192) if rt else None
+        for word in text.split():
+            c, i = word[0], int(word[1:])
+            if c == "A":
+                act(B("DY", i, 2048), G(xw, B("o4", i, 128)))
+            elif c == "D":
+                for k in (2 * i, 2 * i + 1):
+                    tt(B("DY", k, 1024), G(xw, B("o4", k, 64)), A("XO", 0, 1024), OP.subtract)
+            elif c == "S":
+                for h in range(2):
+                    o = B("ps", 2 * (i & 1) + h, 512)
+                    mm(o, Mx(mI), B("DY", 2 * i + h, 512), True, False)
+                    mm(o, Mx(mNI), B("XO", h, 512), False, True)
+            elif c == "P":
+                act(B("AB", 2 * ab(i // 2) + (i & 1), 1024), B("ps", i & 1, 1024), AF.Abs)
+            elif c == "T":
+                red(i, False)
+            elif c == "R":
+                ts(B("AB", ab(i), 2048), B("DY", i, 2048), 0.0, OP.max)
+                red(i, True)
+            elif c == "Q":
+                act(B("AB", ab(i), 2048), B("DY", i, 2048), AF.Abs)
+                red(i, False)
+            elif c == "x" and i == 0:
+                cp(A("kf", 0, 256), PS(3072, 3328))
+                tt(A("kf", 256, 512), A("kf", 0, 256), PS(3328, 3584), OP.max)
+            elif c == "x":
+                tt(A("kf", 0, 256), A("kf", 256, 512), PS(3584, 3840), OP.max)
+                tt(A("kf", 256, 384), A("kf", 0, 128), PS(2048, 2176), OP.max)
+                tt(A("kf", 384, 512), A("kf", 256, 384), A("kf", 128, 256), OP.max)
+                tt(A("kf", 0, 128), A("kf", 384, 512), PS(2560, 2688), OP.max)
+            elif c == "a":
+                gslot[i] = B("AB", st["ag"] % 6, 1024)
+                st["ag"] += 1
+                act(gslot[i], G(rw, B(off, i, 64)))
+            elif c == "j" and i == 0:
+                for h in range(2):
+                    mm(B("ps", h, 512), Mx(mT0), B("VER", h, 512), True, False)
+                    mm(B("ps", h, 512), Mx(mT1), B("VER", 2 + h, 512), False, True)
+                act(A("jb", 0, 1024), PS(0, 1024), AF.Identity, bias=EIGHTH, scale=0.125)
+            elif c == "j" and i < 3:
+                for h in range(2):
+                    o = B("ps", 2 + h, 512)
+                    if i == 1:
+                        mm(o, Mx(mI), B("N2", 2 + h, 512), True, False)
+                    else:
+                        mm(o, Mx(mT0), B("VER", h, 512), True, False)
+                        mm(o, Mx(mT1), B("VER", 2 + h, 512), False, False)
+                for h in range(2):
+                    mm(B("ps", 2 + h, 512), Mx(m8), B("jb", h, 512), False, True)
+            elif c == "j":
+                act(A("tA", 0, 1024), PS(1024, 2048), AF.Identity, bias=cf(29), scale=cf(11))
+                act(A("tA", 1024, 2048), PS(1024, 2048), AF.Identity, bias=cf(30), scale=cf(5))
+                act(A("n2N", 0, 1024), PS(1024, 2048), AF.Square, bias=7.0 - 1536, scale=-1.0)
+            elif c == "w":
+                wrapped(i)
+            elif c == "l":
+                digits(i)
+            elif c == "c":
+                first(i)
+            elif c == "b":
+                bnd[i] = bound(i)
+            elif c == "m":
+                tt(B("DY", i, 1024), gslot[i], bnd[i], OP.min)
+                done(i)
+            elif c == "g":
+                tt(B("DY", i, 1024), G(rw, B(off, i, 64)), pre[i], OP.min)
+                done(i)
+            elif c == "o":
+                ts(B("o4", i, 512), B("ps", 6 + i, 512), -7.5, OP.add, 1.0 / 16, OP.mult)
+                ts(B("o3b", i, 512), B("ps", 6 + i, 512), -3.5, OP.add, 0.125, OP.mult)
+            elif c == "L":
+                act(B("VER", i, 1024), PS(2048, 3072))
+                versions([i])
+
+    sf = lambda k: B("sf", k, 64)
+    si = lambda k: B("si", k, 64)
+    su = lambda k: B("su", k, 64)
+
+    def table(t):
+        mm(PS(3072, 3200), A("kf", 0, 128), A("I32m", 0, 128), True, True)
+        cp(sf(0), PS(3072, 3136))
+        tt(si(0), sf(0), PS(3136, 3200), OP.max)
+        ts(si(1), si(0), 1, AND)
+        ts(si(2), si(0), 15, AND)
+        cp(A("sb", 0, 64), si(1))
+        mm(PS(3584, 3648), Mx(mOne), A("sb", 0, 64), True, True)
+        add("v", lambda: g.vector.tensor_reduce(cf(32)[0], PS(3584, 3648)[0], AxisListType.X, OP.add), [PS(3584, 3648)], [cf(32)])
+        ts(si(3), si(2), cf(32), OP.add, 2048.0, OP.mult)
+        ts(si(4), si(3), 15 * 2048, AND)
+        ts(sf(2), si(4), 15000.0, OP.is_gt, 17408.0, OP.mult)
+        tt(sf(6), A("Wv", 128, 192), si(4), OP.subtract)
+        ts(sf(3), si(4), 30000.0, OP.is_gt, 13312.0, OP.mult)
+        ts(sf(4), si(4), 15000.0, OP.is_gt, 15360.0, OP.mult)
+        tt(sf(8), A("Wv", 64, 128), si(4), OP.subtract)
+        tt(sf(7), sf(2), sf(6), OP.add)
+        ts(sf(5), si(4), 30000.0, OP.is_gt, 15360.0, OP.mult)
+        tt(sf(9), sf(4), sf(8), OP.add)
+        tt(sf(12), sf(7), sf(3), OP.add)
+        tt(sf(13), sf(9), sf(5), OP.add)
+        cp(su(1), sf(12))
+        cp(su(0), sf(13))
+        RT = "RT%d" % t
+        ver = A("VER", 0, 16384)
+        c0 = 2048 * rank
+        n = 1024 // PIECES
+        place = lambda h, ch: 512 * (2 * (h & 1) + ch) + n * (h >> 1)
+        for h in range(PIECES + 1):
+            for ch in range(2):
+                if h < PIECES:
+                    ev("va"[ch], B("AB", 2 * h + ch, n), G(ver, B("su", PIECES * ch + h, n // 16)))
+                    mm(PS(place(h, ch), place(h, ch) + n), Mx(mDF), B("AB", 2 * h + ch, n), True, True)
+            if h > 0:
+                for ch in range(2):
+                    k = c0 + 2 * n * (h - 1)
+                    ev("va"[ch], A(RT, k + ch, k + 2 * n, 2, reg=(k + n * ch, k + n * ch + n)),
+                       PS(place(h - 1, ch), place(h - 1, ch) + n))
+                out_piece(RT, 2048, PIECES, t, h - 1)
+        hand_on(RT, 2048, PIECES, t)
+        st["tile"] = 0
+        abslot.clear()
+
+    def lists(lo, hi):
+        ts(sf(10), si(2), -1024.0, OP.mult)
+        ts(sf(11), si(2), hi, OP.is_gt, 1024.0, OP.mult)
+        ts(sf(1), si(2), lo, OP.is_lt, 1024.0, OP.mult)
+        tt(sf(14), sf(10), A("Wv", 64, 128), OP.add)
+        tt(sf(15), sf(11), A("Wv", 0, 64), OP.add)
+        cp(su(2), sf(14))
+        tt(sf(0), sf(15), sf(1), OP.add)
+        cp(su(3), sf(0))
+        act(A("Zh", 0, 1024), G(A("DY", 0, 16384), su(2)), scale=0.5)
+
+    def newx(out):
+        tt(A("sm", 0, 1024), G(A("W2", 0, 2048), su(3)), A("Zh", 0, 1024), OP.add)
+        ts(out, A("sm", 0, 1024), R1, OP.add, R1, OP.subtract)
+
+    vports = lambda text: [int(w[1:]) for w in text.split() if w[0] == "g"]
+
+    steps(VOTE1, "XT0", None, None, None)
+    table(0)
+    lists(-1.0, 9.5)
+    consts2()
+    vp = vports(MIDDLE)
+    premade(vp[0], "a", 0)
+    premade(vp[1], "a", 1)
+    for i in range(16):
+        mm(PS(2048 + 64 * i, 2112 + 64 * i), A("T2", 128 * i, 128 * i + 128, reg=(0, 2048)), Mx(mWl, 64), True, True)
+    act(A("jw", 0, 1024), PS(2048, 3072), AF.Identity, bias=EIGHTH, scale=0.125)
+    newx(B("XT1", rank, 1024))
+    premade(vp[2], "a", 0)
+    for h in range(2):
+        mm(B("ps", 6 + h, 512), Mx(m8), B("jw", h, 512), True, False)
+        for i in range(8 * h, 8 * h + 8):
+            mm(PS(3072 + 64 * i, 3136 + 64 * i), A("T2", 128 * i, 128 * i + 128, reg=(0, 2048)), Mx(mWl, 64), False, i % 8 == 7)
+    premade(vp[3], "v", 1)
+    premade(vp[4], "v", 2)
+    act(A("n2W", 0, 1024), PS(3072, 4096), AF.Square, bias=7.0 - 1536, scale=-1.0)
+    for k, i in enumerate(vp[5:]):
+        premade(i, "av"[k & 1], (0, 1, 3, 2)[k & 3])
+    share_x("XT1", "ax1")
+    dma("s", A("XO", 0, 1024), B("XT1", rank, 1024))
+    steps(MIDDLE, "XT1", "RT0", "o3", done1)
+    table(1)
+    lists(2.0 * len([w for w in MIDDLE.split() if w[0] == "A"]) - 6.5, 9.5)
+    act(A("W2", 0, 1024), A("XO", 0, 1024), AF.Identity, bias=-0.25)
+    act(A("W2", 1024, 2048), A("XO", 0, 1024), AF.Identity, bias=-0.25, scale=0.5)
+    pre.clear()
+    fin.clear()
+    vp = vports(LAST)
+    for k, i in enumerate(vp):
+        premade(i, "vvvaa"[k], k & 3)
+    newx(A("X2", 0, 1024))
+    dma("s", hbm(T.yx, 0, 1024), A("X2", 0, 1024))
+    steps(LAST, None, "RT1", "o3b", done2)
+    for h in range(2):
+        ev("av"[h], B("sm", h, 512), B("ps", 4 + h, 512))
+        dma("as"[h], hbm(T.yr, 512 * h, 512 * h + 512), B("sm", h, 512))
+
+    emit(g, T, Q, ops)
+
+
+def arrange(ops):
+    n = len(ops)
+    before = [set(o["deps"]) | o["chain"] for o in ops]
+    last = {}
+    for k, o in enumerate(ops):
+        if o["q"] in KEEP or o["kind"] == "d":
+            if o["q"] in last:
+                before[k].add(last[o["q"]])
+            last[o["q"]] = k
+        if o["kind"] == "r":
+            last["r"] = k
+        if o["kind"] == "x":
+            before[k].add(last["r"])
+    after = [[] for _ in ops]
+    for k in range(n):
+        for m in before[k]:
+            after[m].append(k)
+    lag = lambda m, k: 0 if (ops[m]["q"] == ops[k]["q"] and m not in ops[k]["deps"]) else ops[m]["lat"]
+    level = [0.0] * n
+    for k in range(n - 1, -1, -1):
+        level[k] = ops[k]["cost"] + max([lag(k, j) + level[j] for j in after[k]] + [ops[k]["lat"]])
+    left = [len(b) for b in before]
+    ready = [0.0] * n
+    cand = {}
+    free = {}
+    for k in range(n):
+        if not left[k]:
+            cand.setdefault(ops[k]["q"], []).append(k)
+    order = []
+    while len(order) < n:
+        best = None
+        for q, cs in cand.items():
+            if not cs:
+                continue
+            f = free.get(q, 0.0) if q else 0.0
+            t0 = min(max(f, ready[k]) for k in cs)
+            k = max((c for c in cs if max(f, ready[c]) <= t0 + WINDOW), key=lambda c: (level[c] - SLOPE * c, -c))
+            if best is None or t0 < best[0]:
+                best = (t0, max(f, ready[k]), k)
+        _, t, k = best
+        q = ops[k]["q"]
+        cand[q].remove(k)
+        free[q] = t + ops[k]["cost"]
+        order.append(ops[k])
+        for j in after[k]:
+            ready[j] = max(ready[j], t + ops[k]["cost"] + lag(k, j))
+            left[j] -= 1
+            if not left[j]:
+                cand.setdefault(ops[j]["q"], []).append(j)
+    return order
+
+
+def emit(g, T, Q, ops):
+    depend(ops)
+    if WINDOW >= 0:
+        ops = arrange(ops)
+        depend(ops)
+    issue(g, T, Q, ops)
+
+
+def depend(ops):
+    acc = {}
+    for n, o in enumerate(ops):
+        deps = set()
+        o["chain"] = set()
+        mine = []
+        for w, rs in ((False, o["rd"]), (True, o["wr"])):
+            for name, lo, hi in rs:
+                if name == "ps":
+                    mine.append((name, lo // 512 * 512, -(-hi // 512) * 512, w, lo, hi))
+                else:
+                    mine.append((name, lo, hi, w, lo, hi))
+        for name, lo, hi, w, l2, h2 in mine:
+            for (m, lo1, hi1, w1, l1, h1) in acc.get(name, []):
+                if lo1 >= hi or lo >= hi1:
+                    continue
+                q1 = ops[m]["q"]
+                if name == "ps":
+                    if q1 == o["q"] and (q1 == "t" or not (w or w1) or l1 >= h2 or l2 >= h1):
+                        o["chain"].add(m)
+                        continue
+                elif not (w or w1):
+                    continue
+                deps.add(m)
+        for name, lo, hi, w, l2, h2 in mine:
+            lst = acc.setdefault(name, [])
+            if w and name != "ps":
+                lst[:] = [e for e in lst if not (lo <= e[1] and e[2] <= hi)]
+            elif name == "ps":
+                lst[:] = [e for e in lst if not (lo <= e[1] and e[2] <= hi and (ops[e[0]]["q"] != o["q"] or o["q"] == "t"))]
+            lst.append((n, lo, hi, w, l2, h2))
+        o["deps"] = deps
+
+
+def issue(g, T, Q, ops):
+    known = {q: {} for q in Q}
+    snap = {}
+    need = set()
+    for n, o in enumerate(ops):
+        if o["kind"] == "x":
+            snap[n] = {}
+            continue
+        kn = known[o["q"]]
+        best = {}
+        for m in o["deps"]:
+            key = ops[m]["q"] if ops[m]["kind"] == "c" else ("e", m)
+            best[key] = max(best.get(key, -1), m)
+        waits = []
+        for key, m in sorted(best.items(), key=lambda kv: -kv[1]):
+            if kn.get(key, -1) >= m:
+                continue
+            waits.append(m)
+            need.add(m)
+            kn[key] = m
+            for k2, m2 in snap[m].items():
+                if kn.get(k2, -1) < m2:
+                    kn[k2] = m2
+        o["waits"] = waits
+        snap[n] = dict(kn)
+    cnt = {q: 0 for q in Q}
+    total = {}
+    for n, o in enumerate(ops):
+        if o["kind"] == "x":
+            o["at"] = (o["sem"], o["n"])
+            total[o["sem"]] = o["n"]
+            continue
+        q = Q[o["q"]]
+        for m in o["waits"]:
+            s, v = ops[m]["at"]
+            q.wait_ge(T.sem[s], v)
+        if o["kind"] == "r":
+            o["fn"](T.sem[o["sem"]])
+            o["at"] = (o["sem"], o["n"])
+            total[o["sem"]] = o["n"]
+        elif o["kind"] == "d":
+            o["fn"]().then_inc(T.sem[o["sem"]], 16)
+            o["at"] = (o["sem"], 16)
+            total[o["sem"]] = 16
+        else:
+            ins = o["fn"]()
+            if n in need:
+                cnt[o["q"]] += 1
+                s = "c" + o["q"]
+                ins.then_inc(T.sem[s], 1)
+                o["at"] = (s, cnt[o["q"]])
+                total[s] = cnt[o["q"]]
+    for s in sorted(total):
+        g.wait_ge(T.sem[s], total[s])

@@ -13,10 +13,10 @@ SCRATCH = {
     "XT0": _sb(4096, BF), "XT1": _sb(4096, BF), "RT0": _sb(8192, BF), "RT1": _sb(8192, BF),
     "DY": _sb(16384, BF), "VER": _sb(16384, BF), "AB": _sb(6144, BF), "BP": _sb(9216, BF),
     "rot_i": _sb(1024, I32),
-    "N2": _sb(2048, BF), "T2": _sb(2048, BF), "W2": _sb(2048, F32), "sm": _sb(1024, F32),
+    "N2": _sb(2048, BF), "T2": _sb(2048, BF), "sm": _sb(1024, F32),
     "o4": _sb(1024, U16), "o3": _sb(1024, U16), "o3b": _sb(1024, U16),
     "jb": _sb(1024, BF), "tA": _sb(2048, BF), "n2N": _sb(1024, BF), "n2W": _sb(1024, BF), "jw": _sb(1024, BF),
-    "Zh": _sb(1024, BF), "X2": _sb(1024, BF), "XO": _sb(1024, BF),
+    "Zh": _sb(1024, F32), "X2": _sb(1024, BF), "XO": _sb(2048, BF),
     "kf": _sb(512, F32), "sf": _sb(1024, F32), "si": _sb(512, I32), "sb": _sb(64, BF), "su": _sb(256, U16),
     "ci": _sb(64, I32), "cf": _sb(64, F32), "XI": _sb(144, F32), "XH": _sb(128, F32), "XG": _sb(128, F32),
     "VL": _sb(128, F32), "tm": _sb(384, F32), "Wv": _sb(192, F32), "I32m": _sb(128, F32), "CI": _sb(16, F32),
@@ -27,6 +27,7 @@ SCRATCH = {
 NDMA = 56
 WINDOW, SLOPE, GATHER = 0.0, 0.0, 1.5
 KEEP = ("g", "s", "v", "a")
+GAP1 = "aaavav"
 PIECES = 4
 SEMAPHORES = (["cv", "ca", "ct", "cg"] + ["d%d" % k for k in range(NDMA)]
               + ["ax1"] + ["%s%d%d" % (s, t, h) for s in ("ap", "as", "af") for t in range(3) for h in range(4)])
@@ -35,12 +36,12 @@ R256 = 1.5 * 2.0 ** 31
 R1 = 1.5 * 2.0 ** 23
 EIGHTH = 192 - 0.4375
 
-VOTE1 = ("A0 D3 A1 S0 S1 R3 D4 P0 S2 P1 S3 T0 A2 D5 R5 P2 S4 P3 S5 T1 D6 Q4 x0 D7 P4 P5 T2 j1 Q6 j3 R7 x1")
+VOTE1 = ("A0 D3 y0 A1 S0 S1 R3 D4 P0 S2 P1 S3 T0 A2 D5 R5 P2 S4 P3 S5 T1 D6 Q4 D7 x0 P4 P5 T2 j1 Q6 R7 x1 y2 j3")
 MIDDLE = ("b3 b4 c0 c2 a3 a4 g0 l0 a5 m3 b5 l3 g1 w0 l1 a6 m4 b6 l4 a7 m5 b7 w2 g2 w1 a14 m6 b14 a15 m7 w3 b15 l5 l2 l6 l7 "
-          "a13 g8 o0 A0 L0 m14 b13 g9 w4 A1 m15 w7 m13 c1 l8 l9 S0 S1 l14 l15 l13 g10 l10 g11 w5 P0 P1 l11 S2 A2 g12 l12 w6 "
-          "L1 S3 T0 D3 P2 S4 P3 S5 T1 o1 R3 P4 P5 T2 A7 D4 S14 S15 x0 D5 Q4 P14 P15 T7 D6 Q5 j0 j2 j3 R6 x1")
+          "a13 g8 o0 L0 a12 m14 b13 A0 c1 l8 l14 g9 w4 l9 m15 w7 b12 l15 m13 l13 g10 l10 m12 w6 l12 S0 S1 A1 g11 w5 l11 "
+          "D3 R3 P0 S2 P1 S3 T0 L1 o1 A2 D4 P2 S4 P3 S5 T1 R4 A7 D5 x0 P4 S14 P5 S15 T2 D6 P14 P15 T7 Q5 j0 j2 j3 R6 x1")
 LAST = ("c3 a3 b3 a4 b4 g0 a5 m3 b5 g1 a6 m4 b6 a7 m5 b7 g2 a10 m6 b10 a11 m7 b11 g8 a12 m10 b12 a13 m11 b13 g9 "
-        "a14 m12 b14 a15 m13 b15 m14 m15")
+        "a14 m12 b14 a15 m13 b15 n14")
 
 
 def rank_program(g, core, T, topo):
@@ -228,43 +229,38 @@ def rank_program(g, core, T, topo):
     ts(cf(11), cf(5), -1.0, OP.mult, 1.0, OP.add)
     ts(cf(23), cf(1), 8.0, EQ)
     ts(cf(24), cf(1), 0.0, EQ)
+    ts(cf(22), cf(1), 14.0, OP.is_lt)
     ts(Mx(mI), XI(128), cf(0), EQ)
-    ts(Mx(mWc, 64), XI(64), cf(3), EQ)
     ts(Mx(mPig), XI(128), cf(8), EQ)
-    ts(A("cf", 25, 27), A("cf", 23, 25), -512.0, OP.mult, 512.0, OP.add)
-    ts(A("CI", 0, 8), XI(8), cf(1), EQ, cf(23), OP.add)
-    ts(A("CI", 8, 16), A("XI", 8, 16), cf(1), EQ, cf(24), OP.add)
-    ts(A("tm", 256, 384), A("XG", 0, 128), cf(2), EQ)
+    lin = lambda k, a, scale, bias: act(cf(k), cf(a), AF.Identity, bias=bias, scale=scale)
+    for k, a, scale, bias in ((10, 9, 2.0, 0.0), (12, 9, 2.0, 1.0), (13, 11, 1.0 / 256, 0.0), (14, 5, 1.0 / 256, 0.0),
+                              (15, 2, 16.0, 15.0), (33, 2, 16.0, 14.0), (34, 2, 16.0, 0.0), (35, 2, 16.0, 8.0),
+                              (21, 0, 1.0, 2.0), (25, 23, -512.0, 512.0), (26, 24, -512.0, 512.0),
+                              (29, 11, 1535.0, 1.0), (30, 5, 1535.0, 1.0), (31, 0, 1.0, -64.0), (16, 6, 255.0, 1.0),
+                              (18, 6, -1.0, 1.0), (27, 11, 256.0, 0.0), (28, 5, 256.0, 0.0),
+                              (17, 6, 1.0, cf(33)), (19, 7, 1.0, cf(34)), (20, 7, 1.0, cf(35))):
+        lin(k, a, scale, bias)
     for h in range(2):
-        ts(B("tm", h, 128), A("VL", 0, 128), cf(23 + h), OP.mult, cf(25 + h), OP.add)
-    for h in range(2):
-        tt(Mx(mGV0 + h), B("tm", h, 128), A("tm", 256, 384), OP.mult)
+        act(B("tm", h, 128), A("VL", 0, 128), AF.Identity, bias=cf(25 + h), scale=cf(23 + h))
     act(Mx(mNI), Mx(mI), scale=-1.0)
     act(A("I32m", 0, 128), Mx(mI))
     act(Mx(m256), Mx(mI), scale=256.0)
     act(Mx(m8), Mx(mI), scale=-8.0)
     act(Mx(m64k), Mx(mI), scale=65536.0)
-    act(A("W2", 0, 1024), A("XO", 0, 1024), AF.Identity, bias=-0.25)
-    act(A("W2", 1024, 2048), A("XO", 0, 1024), AF.Identity, bias=-0.25, scale=0.5)
+    act(A("XO", 1024, 2048), A("XO", 0, 1024), scale=0.5)
     for h in range(2):
         ts(B("N2", h, 512), B("rot_i", h, 512), R256, OP.add, R256, OP.subtract)
     for h in range(2):
         tt(B("N2", 2 + h, 512), B("rot_i", h, 512), B("N2", h, 512), OP.subtract)
-    for i in range(16):
-        act(B("WB", i, 128), Mx(mGV0 + i // 8), scale=col("CI", i))
-    ts(cf(10), cf(9), 2.0, OP.mult)
-    ts(cf(12), cf(9), 2.0, OP.mult, 1.0, OP.add)
-    ts(cf(13), cf(11), 1.0 / 256, OP.mult)
-    ts(cf(14), cf(5), 1.0 / 256, OP.mult)
+    act(A("jb", 0, 1024), A("N2", 1024, 2048), AF.Identity, bias=EIGHTH, scale=0.125)
+    ts(Mx(mWc, 64), XI(64), cf(3), EQ)
     ts(Mx(mL00), XI(128), cf(10), EQ, cf(11), OP.mult)
     ts(Mx(mL01), XI(128), cf(12), EQ, cf(13), OP.mult)
     ts(Mx(mL10), XI(128), cf(10), EQ, cf(5), OP.mult)
     ts(Mx(mL11), XI(128), cf(12), EQ, cf(14), OP.mult)
-    ts(cf(15), cf(2), 16.0, OP.mult, 15.0, OP.add)
-    ts(cf(21), cf(0), 2.0, OP.add)
-    ts(cf(22), cf(1), 14.0, OP.is_lt)
-    act(cf(29), cf(11), AF.Identity, bias=1.0, scale=1535.0)
-    act(cf(30), cf(5), AF.Identity, bias=1.0, scale=1535.0)
+    for k, w in enumerate((32.0, -16.0, 16.0)):
+        ts(B("Wg", k, 8), XI(8), cf(2), EQ, w, OP.mult)
+    add("v", lambda: g.vector.memset(Mx(mOne)[0], 1.0), [], [Mx(mOne)])
     for b in range(16):
         mm(PS(128 * b, 128 * b + 128), A("N2", b, 2048, 16, reg=(0, 2048)), Mx(mPig), True, True)
     for bank in (0, 1, 2, 3):
@@ -277,23 +273,38 @@ def rank_program(g, core, T, topo):
             o = B("ps", 2 * ch + h, 512)
             mm(o, Mx(mL00 + 2 * ch), B("N2", 2 + h, 512), True, False)
             mm(o, Mx(mL01 + 2 * ch), B("N2", h, 512), False, True)
-    ts(A("tm", 1, 8), A("ci", 9, 16), -2.0, OP.mult, cf(0), OP.add)
-    ts(A("tm", 8, 16), XI(8), 2.0, OP.mult)
-    for k, w in enumerate((32.0, -16.0, 16.0)):
-        ts(B("Wg", k, 8), XI(8), cf(2), EQ, w, OP.mult)
-    tt(A("PI", 1, 8), A("tm", 1, 8), A("tm", 9, 16), OP.add)
-    add("v", lambda: g.vector.memset(Mx(mOne)[0], 1.0), [], [Mx(mOne)])
+    ts(A("cf", 41, 48), A("ci", 9, 16), -2.0, OP.mult, cf(0), OP.add)
+    ts(A("cf", 48, 56), XI(8), 2.0, OP.mult)
     ts(A("Wv", 0, 64), A("Wv", 0, 64), cf(15), OP.subtract, 15.0, OP.add)
+    tt(A("PI", 1, 8), A("cf", 41, 48), A("cf", 49, 56), OP.add)
     ts(Mx(mWl), XI(128), cf(21), EQ, cf(22), OP.mult)
-    act(A("jb", 0, 1024), A("N2", 1024, 2048), AF.Identity, bias=EIGHTH, scale=0.125)
-    for h in range(2):
-        ts(B("o4", h, 512), B("ps", 4 + h, 512), -7.5, OP.add, 1.0 / 16, OP.mult)
+
+    def first_offsets(h):
+        ts(B("o3", h, 512), B("ps", 4 + h, 512), -3.5, OP.add, 0.125, OP.mult)
+        ts(B("o4", h, 512), B("o3", h, 512), -0.5, OP.add, 0.5, OP.mult)
+
+    first_offsets(0)
     for ch in range(2):
         act(B("VER", ch, 1024), B("ps", ch, 1024))
-    ts(A("o3", 0, 1024), PS(2048, 3072), -3.5, OP.add, 0.125, OP.mult)
-    tt(Mx(mDF), Mx(mI), Mx(mWl), OP.subtract)
-    act(A("Wv", 64, 128), A("Wv", 0, 64), AF.Identity, bias=15360.0)
-    act(A("Wv", 128, 192), A("Wv", 0, 64), AF.Identity, bias=14336.0)
+
+    def bound_weights(part):
+        if part == 0:
+            first_offsets(1)
+            tt(Mx(mDF), Mx(mI), Mx(mWl), OP.subtract)
+        elif part == 1:
+            ts(A("tm", 256, 384), A("XG", 0, 128), cf(2), EQ)
+            ts(A("CI", 0, 8), XI(8), cf(1), EQ, cf(23), OP.add)
+            ts(A("CI", 8, 16), A("XI", 8, 16), cf(1), EQ, cf(24), OP.add)
+            later.pop(0)()
+        elif part == 4:
+            for h in range(2):
+                tt(Mx(mGV0 + h), B("tm", h, 128), A("tm", 256, 384), OP.mult)
+        elif part == 2:
+            act(A("Wv", 64, 128), A("Wv", 0, 64), AF.Identity, bias=15360.0)
+            act(A("Wv", 128, 192), A("Wv", 0, 64), AF.Identity, bias=14336.0)
+        else:
+            for i in range(16):
+                act(B("WB", i, 128), Mx(mGV0 + i // 8), scale=col("CI", i))
 
     def versions(hs):
         for h in hs:
@@ -307,22 +318,13 @@ def rank_program(g, core, T, topo):
 
     versions([0, 1])
 
-    def consts2():
-        ts(cf(31), cf(0), -64.0, OP.add)
-        ts(Mx(mWl, 64), XI(64), cf(31), EQ)
-        ts(cf(16), cf(6), 255.0, OP.mult, 1.0, OP.add)
-        ts(cf(18), cf(6), -1.0, OP.mult, 1.0, OP.add)
-        ts(cf(27), cf(11), 256.0, OP.mult)
-        ts(cf(28), cf(5), 256.0, OP.mult)
-        ts(cf(17), cf(15), -1.0, OP.add, cf(6), OP.add)
-        ts(cf(19), cf(15), -15.0, OP.add, cf(7), OP.add)
-        ts(cf(20), cf(15), -7.0, OP.add, cf(7), OP.add)
-        ts(A("Zw", 0, 144), XI(144), cf(15), EQ, cf(16), OP.mult)
-        ts(A("Z2", 0, 144), XI(144), cf(17), EQ)
-        ts(Mx(mC0), A("XH", 0, 128), cf(9), EQ, cf(27), OP.mult)
-        ts(Mx(mC1), A("XH", 0, 128), cf(9), EQ, cf(28), OP.mult)
-        ts(Mx(mT0), XI(128), cf(19), EQ, cf(18), OP.mult)
-        ts(Mx(mT1), XI(128), cf(20), EQ, cf(18), OP.mult)
+    later = [lambda: ts(Mx(mWl, 64), XI(64), cf(31), EQ),
+             lambda: ts(A("Zw", 0, 144), XI(144), cf(15), EQ, cf(16), OP.mult),
+             lambda: ts(A("Z2", 0, 144), XI(144), cf(17), EQ),
+             lambda: ts(Mx(mC0), A("XH", 0, 128), cf(9), EQ, cf(27), OP.mult),
+             lambda: ts(Mx(mC1), A("XH", 0, 128), cf(9), EQ, cf(28), OP.mult),
+             lambda: ts(Mx(mT0), XI(128), cf(19), EQ, cf(18), OP.mult),
+             lambda: ts(Mx(mT1), XI(128), cf(20), EQ, cf(18), OP.mult)]
 
     slot = [3072, 3200, 3328, 3456, 3584, 3712, 2048, 2560]
     st = {"tile": 0, "ab": 0, "nb": 1, "ag": 0}
@@ -443,6 +445,8 @@ def rank_program(g, core, T, topo):
                 act(A("tA", 0, 1024), PS(1024, 2048), AF.Identity, bias=cf(29), scale=cf(11))
                 act(A("tA", 1024, 2048), PS(1024, 2048), AF.Identity, bias=cf(30), scale=cf(5))
                 act(A("n2N", 0, 1024), PS(1024, 2048), AF.Square, bias=7.0 - 1536, scale=-1.0)
+            elif c == "y":
+                bound_weights(i)
             elif c == "w":
                 wrapped(i)
             elif c == "l":
@@ -454,12 +458,20 @@ def rank_program(g, core, T, topo):
             elif c == "m":
                 tt(B("DY", i, 1024), gslot[i], bnd[i], OP.min)
                 done(i)
+            elif c == "n":
+                for h in range(2):
+                    for k in (i, i + 1):
+                        s, b = gslot[k][1][1] + 512 * h, bnd[k][1][1] + 512 * h
+                        tt(B("DY", 2 * k + h, 512), A("AB", s, s + 512), PS(b, b + 512), OP.min)
+                        mm(B("ps", 4 + h, 512), A("Zw", 15 - k, 143 - k), B("DY", 2 * k + h, 512), False, k > i)
+                    ev("a", B("sm", h, 512), B("ps", 4 + h, 512))
+                    dma("s", hbm(T.yr, 512 * h, 512 * h + 512), B("sm", h, 512))
             elif c == "g":
                 tt(B("DY", i, 1024), G(rw, B(off, i, 64)), pre[i], OP.min)
                 done(i)
             elif c == "o":
-                ts(B("o4", i, 512), B("ps", 6 + i, 512), -7.5, OP.add, 1.0 / 16, OP.mult)
                 ts(B("o3b", i, 512), B("ps", 6 + i, 512), -3.5, OP.add, 0.125, OP.mult)
+                ts(B("o4", i, 512), B("o3b", i, 512), -0.5, OP.add, 0.5, OP.mult)
             elif c == "L":
                 act(B("VER", i, 1024), PS(2048, 3072))
                 versions([i])
@@ -470,12 +482,17 @@ def rank_program(g, core, T, topo):
 
     def table(t):
         mm(PS(3072, 3200), A("kf", 0, 128), A("I32m", 0, 128), True, True)
+        if t == 0:
+            bound_weights(1)
         cp(sf(0), PS(3072, 3136))
         tt(si(0), sf(0), PS(3136, 3200), OP.max)
         ts(si(1), si(0), 1, AND)
         ts(si(2), si(0), 15, AND)
         cp(A("sb", 0, 64), si(1))
         mm(PS(3584, 3648), Mx(mOne), A("sb", 0, 64), True, True)
+        if t == 0:
+            bound_weights(4)
+            bound_weights(3)
         add("v", lambda: g.vector.tensor_reduce(cf(32)[0], PS(3584, 3648)[0], AxisListType.X, OP.add), [PS(3584, 3648)], [cf(32)])
         ts(si(3), si(2), cf(32), OP.add, 2048.0, OP.mult)
         ts(si(4), si(3), 15 * 2048, AND)
@@ -520,42 +537,39 @@ def rank_program(g, core, T, topo):
         cp(su(2), sf(14))
         tt(sf(0), sf(15), sf(1), OP.add)
         cp(su(3), sf(0))
-        act(A("Zh", 0, 1024), G(A("DY", 0, 16384), su(2)), scale=0.5)
+        act(A("Zh", 0, 1024), G(A("DY", 0, 16384), su(2)), AF.Identity, bias=-0.25, scale=0.5)
 
     def newx(out):
-        tt(A("sm", 0, 1024), G(A("W2", 0, 2048), su(3)), A("Zh", 0, 1024), OP.add)
+        tt(A("sm", 0, 1024), G(A("XO", 0, 2048), su(3)), A("Zh", 0, 1024), OP.add)
         ts(out, A("sm", 0, 1024), R1, OP.add, R1, OP.subtract)
 
     vports = lambda text: [int(w[1:]) for w in text.split() if w[0] == "g"]
 
     steps(VOTE1, "XT0", None, None, None)
     table(0)
-    lists(-1.0, 9.5)
-    consts2()
     vp = vports(MIDDLE)
-    premade(vp[0], "a", 0)
-    premade(vp[1], "a", 1)
     for i in range(16):
         mm(PS(2048 + 64 * i, 2112 + 64 * i), A("T2", 128 * i, 128 * i + 128, reg=(0, 2048)), Mx(mWl, 64), True, True)
     act(A("jw", 0, 1024), PS(2048, 3072), AF.Identity, bias=EIGHTH, scale=0.125)
-    newx(B("XT1", rank, 1024))
-    premade(vp[2], "a", 0)
+    lists(-1.0, 9.5)
+    premade(vp[0], "v", 0)
+    premade(vp[1], "v", 1)
     for h in range(2):
         mm(B("ps", 6 + h, 512), Mx(m8), B("jw", h, 512), True, False)
         for i in range(8 * h, 8 * h + 8):
             mm(PS(3072 + 64 * i, 3136 + 64 * i), A("T2", 128 * i, 128 * i + 128, reg=(0, 2048)), Mx(mWl, 64), False, i % 8 == 7)
-    premade(vp[3], "v", 1)
-    premade(vp[4], "v", 2)
     act(A("n2W", 0, 1024), PS(3072, 4096), AF.Square, bias=7.0 - 1536, scale=-1.0)
-    for k, i in enumerate(vp[5:]):
-        premade(i, "av"[k & 1], (0, 1, 3, 2)[k & 3])
+    newx(B("XT1", rank, 1024))
+    for k, i in enumerate(vp[2:]):
+        premade(i, GAP1[k], (2, 0, 1, 3)[k & 3])
+    while later:
+        later.pop(0)()
     share_x("XT1", "ax1")
     dma("s", A("XO", 0, 1024), B("XT1", rank, 1024))
     steps(MIDDLE, "XT1", "RT0", "o3", done1)
     table(1)
     lists(2.0 * len([w for w in MIDDLE.split() if w[0] == "A"]) - 6.5, 9.5)
-    act(A("W2", 0, 1024), A("XO", 0, 1024), AF.Identity, bias=-0.25)
-    act(A("W2", 1024, 2048), A("XO", 0, 1024), AF.Identity, bias=-0.25, scale=0.5)
+    act(A("XO", 1024, 2048), A("XO", 0, 1024), scale=0.5)
     pre.clear()
     fin.clear()
     vp = vports(LAST)
@@ -564,9 +578,6 @@ def rank_program(g, core, T, topo):
     newx(A("X2", 0, 1024))
     dma("s", hbm(T.yx, 0, 1024), A("X2", 0, 1024))
     steps(LAST, None, "RT1", "o3b", done2)
-    for h in range(2):
-        ev("av"[h], B("sm", h, 512), B("ps", 4 + h, 512))
-        dma("as"[h], hbm(T.yr, 512 * h, 512 * h + 512), B("sm", h, 512))
 
     emit(g, T, Q, ops)
 

@@ -10,38 +10,33 @@ def _sb(n, d):
 
 SCRATCH = {
     "ps": ("psum", [128, 4096], F32),
-    "XT0": _sb(4096, BF), "XT1": _sb(4096, BF), "RT0": _sb(8192, BF), "RT1": _sb(8192, BF),
-    "DY": _sb(16384, BF), "VER": _sb(16384, BF), "AB": _sb(6144, BF), "BP": _sb(9216, BF),
-    "rot_i": _sb(1024, I32),
-    "N2": _sb(2048, BF), "T2": _sb(2048, BF), "sm": _sb(1024, F32),
-    "o4": _sb(1024, U16), "o3": _sb(1024, U16), "o3b": _sb(1024, U16),
-    "jb": _sb(1024, BF), "tA": _sb(2048, BF), "n2N": _sb(1024, BF), "n2W": _sb(1024, BF), "jw": _sb(1024, BF),
-    "Zh": _sb(1024, F32), "X2": _sb(1024, BF), "XO": _sb(2048, BF),
+    "BIG": _sb(81920, BF), "XT1": _sb(4096, BF), "ST1": _sb(8192, BF),
+    "rot_i": _sb(1024, I32), "hu": _sb(1024, U16), "o4": _sb(1024, U16), "oq": _sb(1024, U16),
+    "sm": _sb(1024, F32), "Zh": _sb(1024, F32), "X2": _sb(1024, BF), "XO": _sb(2048, BF),
     "kf": _sb(512, F32), "sf": _sb(1024, F32), "si": _sb(512, I32), "sb": _sb(64, BF), "su": _sb(256, U16),
-    "ci": _sb(64, I32), "cf": _sb(64, F32), "XI": _sb(144, F32), "XH": _sb(128, F32), "XG": _sb(128, F32),
-    "VL": _sb(128, F32), "tm": _sb(384, F32), "Wv": _sb(192, F32), "I32m": _sb(128, F32), "CI": _sb(16, F32),
-    "M": _sb(20 * 128, BF), "WB": _sb(2048, BF), "Zw": _sb(144, BF), "Z2": _sb(144, BF), "Wg": _sb(32, BF),
-    "CT": _sb(1024, BF), "PI": _sb(16, I32),
+    "ci": _sb(64, I32), "cf": _sb(64, F32), "XI": _sb(144, F32), "Wv": _sb(192, F32), "I32m": _sb(128, F32),
+    "M": _sb(8 * 128, BF), "Z": _sb(4 * 144, BF), "Wg": _sb(32, BF), "CT": _sb(1024, BF), "PI": _sb(16, I32),
     "LD": ("dram", [128, 2048], BF),
 }
-NDMA = 56
-WINDOW, SLOPE, GATHER = 0.0, 0.0, 1.5
+PART = {"TB": 0, "XT0": 0, "N2": 4096, "T2": 6144, "NB0": 8192, "FILL": 10240, "AB": 14336, "DY": 30720, "VER": 47104,
+        "OUT": 65536, "ST0": 65536, "NB1": 79872}
+NDMA = 64
+WINDOW, SLOPE, GATHER = 0.0, 0.0, 1.3
 KEEP = ("g", "s", "v", "a")
-GAP1 = "aaavav"
 PIECES = 4
-SEMAPHORES = (["cv", "ca", "ct", "cg"] + ["d%d" % k for k in range(NDMA)]
+NV = 1024 // PIECES
+SEMAPHORES = (["cv", "ca", "ct", "cg", "lay0", "lay1", "ld0", "ld1", "yout"] + ["d%d" % k for k in range(NDMA)]
               + ["ax1"] + ["%s%d%d" % (s, t, h) for s in ("ap", "as", "af") for t in range(3) for h in range(4)])
-(mI, mNI, m256, m64k, mPig, mWc, mL00, mL01, mL10, mL11, mC0, mC1, mT0, mT1, mDF, mOne, mGV0, mGV1, mWl, m8) = range(20)
-R256 = 1.5 * 2.0 ** 31
+mI, mNI, mPig, mWc, mOne, mK, mW1, mW3 = range(8)
 R1 = 1.5 * 2.0 ** 23
-EIGHTH = 192 - 0.4375
+FLOOR = 192 - 0.49
 
-VOTE1 = ("A0 D3 y0 A1 S0 S1 R3 D4 P0 S2 P1 S3 T0 A2 D5 R5 P2 S4 P3 S5 T1 D6 Q4 D7 x0 P4 P5 T2 j1 Q6 R7 x1 y2 j3")
-MIDDLE = ("b3 b4 c0 c2 a3 a4 g0 l0 a5 m3 b5 l3 g1 w0 l1 a6 m4 b6 l4 a7 m5 b7 w2 g2 w1 a14 m6 b14 a15 m7 w3 b15 l5 l2 l6 l7 "
-          "a13 g8 o0 L0 a12 m14 b13 A0 c1 l8 l14 g9 w4 l9 m15 w7 b12 l15 m13 l13 g10 l10 m12 w6 l12 S0 S1 A1 g11 w5 l11 "
-          "D3 R3 P0 S2 P1 S3 T0 L1 o1 A2 D4 P2 S4 P3 S5 T1 R4 A7 D5 x0 P4 S14 P5 S15 T2 D6 P14 P15 T7 Q5 j0 j2 j3 R6 x1")
-LAST = ("c3 a3 b3 a4 b4 g0 a5 m3 b5 g1 a6 m4 b6 a7 m5 b7 g2 a10 m6 b10 a11 m7 b11 g8 a12 m10 b12 a13 m11 b13 g9 "
-        "a14 m12 b14 a15 m13 b15 n14")
+VOTE = "A1 S0 S1 R3 D4 P0 S2 P1 S3 T0 A2 D5 R5 P2 S4 P3 S5 T1 D6 Q4 D7 x0 P4 P5 T2 Q6 R7 x1"
+VOTE1 = "A0 D3 o1 " + VOTE
+PAIRS1 = "g0 a1 w0 g2 a3 w1 g4 a5 w2 g6 a7 w3 g8 a9 w4 g10 o0 a11 w5 g12 a13 w6 g14 a15 w7"
+VOTE2 = "A0 D3 o1 " + VOTE
+PAIRS2 = ("v0-2 a2-4 v4-6 a6-8 ev0-2 ea2-4 y0-4 v8-10 a10-12 ev4-6 ea6-8 y4-8 v12-13 a13-14 ev8-10 ea10-12 y8-12 "
+          "v14-15 a15-16 ev12-13 ea13-14 ev14-15 ea15-16 y12-16")
 
 
 def rank_program(g, core, T, topo):
@@ -57,16 +52,24 @@ def rank_program(g, core, T, topo):
     ndma = [0]
 
     def A(name, lo, hi, step=1, p=None, reg=None):
+        reg = reg if reg else (lo, hi)
+        n = -(-(hi - lo) // step)
+        if name in PART:
+            o = PART[name]
+            name, lo, hi, reg = "BIG", lo + o, hi + o, (reg[0] + o, reg[1] + o)
         t = T[name]
-        ps = slice(0, 128) if p is None else slice(p[0], p[1])
+        ps = slice(0, 128) if p is None else slice(*p)
         ap = t[ps, lo:hi] if step == 1 else t[ps, lo:hi:step]
-        return (ap, (name,) + (reg if reg else (lo, hi)) + (-(-(hi - lo) // step),))
+        return (ap, (name,) + reg + (n,))
 
-    def B(name, k, n):
-        return A(name, n * k, n * k + n)
+    def B(name, k, n, p=None):
+        return A(name, n * k, n * k + n, p=p)
 
-    def Mx(k, n=128):
-        return A("M", 128 * k, 128 * k + n)
+    def Mx(k, n=128, o=0):
+        return A("M", 128 * k + o, 128 * k + o + n)
+
+    def Z(k, lo=0, n=144):
+        return A("Z", 144 * k + lo, 144 * k + lo + n)
 
     def col(name, j):
         return A(name, j, j + 1)
@@ -88,25 +91,25 @@ def rank_program(g, core, T, topo):
         return 0.5 if all(SCRATCH[x[1][0]][2] in (BF, U16) for x in xs) else 1.0
 
     def add(q, fn, rd, wr, kind="c", sem=None, n=1, rate=1.0):
-        if kind in ("d", "r"):
+        if kind in ("d", "r") and sem is None:
             sem = "d%d" % ndma[0]
             ndma[0] += 1
         size = lambda x: x[1][3]
         lat = 90
         if kind == "x":
-            cost, lat = 0, {"p": 6000, "s": 4500, "f": 4000, "x": 11000}[sem[1]]
+            cost, lat = 0, {"p": 5000, "s": 3500, "f": 3000, "x": 9000}[sem[1]]
         elif kind == "r":
             cost, lat = 700, 3000
         elif kind == "d":
-            cost, lat = (1700 if q == "g" else 60), 3500
+            cost, lat = (1700 if q == "g" else 60), 3000
         elif q == "t":
-            cost, lat = max(64, size(rd[1])) * (2.0 if rd[0][1][0] == "kf" else 0.5), 190
+            cost, lat = max(64, size(rd[1])) * (1.7 if rd[0][1][0] == "kf" else 0.42), 190
         elif q == "g":
-            cost = 130 + 2 * size(wr[0])
+            cost = 130 + 1.7 * size(wr[0])
         elif rd and len(rd[0]) == 3:
             cost = 60 + GATHER * 16 * (rd[0][2][2] - rd[0][2][1])
         else:
-            cost = 60 + max(40, size(wr[0]) * rate)
+            cost = 60 + 0.83 * max(64, size(wr[0]) * rate)
         ops.append({"q": q, "fn": fn, "rd": regs(rd), "wr": regs(wr), "kind": kind, "sem": sem, "n": n, "cost": cost, "lat": lat})
 
     def ts(out, in0, s1, o0, s2=None, o1=None):
@@ -122,6 +125,9 @@ def rank_program(g, core, T, topo):
 
     def cp(out, a):
         add("v", lambda: g.vector.tensor_copy(out[0], a[0]), [a], [out])
+
+    def fill(out, c):
+        add("v", lambda: g.vector.memset(out[0], c), [], [out], rate=short(out))
 
     def act(out, a, f=AF.Copy, bias=0.0, scale=1.0):
         add("a", lambda: g.scalar.activation(out[0], a[0], f, bias=val(bias), scale=val(scale)), [a, bias, scale], [out])
@@ -141,13 +147,13 @@ def rank_program(g, core, T, topo):
         else:
             add("g", lambda: g.iota(out[0], pat, base, cm), [], [out])
 
-    def dma(q, out, a):
-        add(q, lambda: Q[q].dma_start(out[0], a[0]), [a], [out], kind="d", n=16)
+    def dma(q, out, a, sem=None):
+        add(q, lambda: Q[q].dma_start(out[0], a[0]), [a], [out], kind="d", n=16, sem=sem)
 
     def nbits(m):
         return bin(m).count("1")
 
-    def send(parts):
+    def send(parts, after=()):
         def fn(ls):
             trs = []
             for v, dst, m, s in parts:
@@ -155,7 +161,7 @@ def rank_program(g, core, T, topo):
                 trs.append(RemoteDMATransfer(dst_ids=[DstId(rid=rid, pnc=pid)], dma_engine_mask=m,
                                              remote_sem=T.sem[s], src=v[0], dst=v[0]))
             g.remote_dma_fused(trs, local_sem=ls)
-        add("g", fn, [v for v, _, _, _ in parts], [], kind="r", n=sum(nbits(m) for _, _, m, _ in parts))
+        add("g", fn, [v for v, _, _, _ in parts] + list(after), [], kind="r", n=sum(nbits(m) for _, _, m, _ in parts))
 
     def arrives(views, sem, n):
         add(None, None, [], views, kind="x", sem=sem, n=n)
@@ -171,10 +177,10 @@ def rank_program(g, core, T, topo):
         e = topo.engines(src, far)
         return sum(1 << k for k in e[:len(e) // 2]), sum(1 << k for k in e[len(e) // 2:])
 
-    def share_x(name, sem):
+    def share_x(name, sem, after):
         mine = B(name, rank, 1024)
         h0, h1 = halves(core)
-        send([(mine, peer, h0, sem), (mine, diag, h1, sem), (mine, sib, split(core)[1], sem)])
+        send([(mine, peer, h0, sem), (mine, diag, h1, sem), (mine, sib, split(core)[1], sem)], after)
         arrives([B(name, T.rank_of(c), 1024) for c in others], sem,
                 nbits(halves(peer)[0]) + nbits(halves(diag)[1]) + nbits(split(sib)[1]))
 
@@ -193,6 +199,7 @@ def rank_program(g, core, T, topo):
 
     PS = lambda lo, hi, step=1, reg=None: A("ps", lo, hi, step, None, reg)
     hbm = lambda t, lo, hi: (t[:, lo:hi], (t.name + "_h", lo, hi))
+    ROWS = (0, 128, 8)
 
     dma("s", B("XT0", 2 * rank, 512), hbm(T.x, 0, 512))
     dma("a", B("XT0", 2 * rank + 1, 512), hbm(T.x, 512, 1024))
@@ -201,66 +208,64 @@ def rank_program(g, core, T, topo):
     dma("s", A("XO", 0, 1024), hbm(T.x, 0, 1024))
     iota(A("ci", 0, 1), [[0, 1]], 0, 1, False)
     iota(A("XI", 0, 144), [[1, 144]], 0, 0)
-    iota(A("XG", 0, 128), [[1, 8], [0, 16]], 0, 0)
-    iota(A("VL", 0, 128), [[0, 8], [-512, 8], [0, 2]], 256, 0)
+    iota(A("CT", 0, 1024, p=(0, 32)), [[-2, 8], [-1, 2], [0, 64]], 15, 0)
     out_piece("XT0", 1024, 2, 2, 0)
     out_piece("XT0", 1024, 2, 2, 1)
     iota(A("Wv", 0, 64), [[16, 64]], 0, 1)
-    iota(A("CT", 0, 1024, p=(0, 32)), [[-2, 8], [-1, 2], [0, 64]], 15, 0)
-    iota(A("XH", 0, 128), [[1, 64], [0, 2]], 0, 0)
     hand_on("XT0", 1024, 2, 2)
     p = col("ci", 0)
     ci = lambda j: col("ci", j)
     cf = lambda j: col("cf", j)
     AND, SHR, EQ = OP.bitwise_and, OP.logical_shift_right, OP.is_equal
     XI = lambda n: A("XI", 0, n)
+    fill(B("FILL", 0, 1024), 0.0)
     ts(ci(1), p, 15, AND)
     ts(ci(2), p, 4, SHR)
     ts(ci(3), p, 63, AND)
     ts(ci(4), p, 7, AND)
     ts(ci(5), p, 3, SHR, 1, AND)
-    ts(ci(6), p, 1, AND)
-    ts(ci(7), p, 1, SHR, 7, AND)
-    for u in range(1, 8):
-        ts(ci(8 + u), p, 2 * u, AND)
+    ts(ci(6), p, 6, SHR)
+    ts(ci(7), p, 0, AND)
+    for u in range(8):
+        ts(ci(8 + u), p, u, AND)
     cp(A("cf", 0, 8), A("ci", 0, 8))
     ts(cf(8), cf(1), 8.0, OP.mult, cf(2), OP.add)
-    ts(cf(9), cf(2), 8.0, OP.mult, cf(4), OP.add)
-    ts(cf(11), cf(5), -1.0, OP.mult, 1.0, OP.add)
-    ts(cf(23), cf(1), 8.0, EQ)
-    ts(cf(24), cf(1), 0.0, EQ)
-    ts(cf(22), cf(1), 14.0, OP.is_lt)
-    ts(Mx(mI), XI(128), cf(0), EQ)
     ts(Mx(mPig), XI(128), cf(8), EQ)
+    ts(Mx(mWc, 64), XI(64), cf(3), EQ)
+    ts(Mx(mI), XI(128), cf(0), EQ)
     lin = lambda k, a, scale, bias: act(cf(k), cf(a), AF.Identity, bias=bias, scale=scale)
-    for k, a, scale, bias in ((10, 9, 2.0, 0.0), (12, 9, 2.0, 1.0), (13, 11, 1.0 / 256, 0.0), (14, 5, 1.0 / 256, 0.0),
-                              (15, 2, 16.0, 15.0), (33, 2, 16.0, 14.0), (34, 2, 16.0, 0.0), (35, 2, 16.0, 8.0),
-                              (21, 0, 1.0, 2.0), (25, 23, -512.0, 512.0), (26, 24, -512.0, 512.0),
-                              (29, 11, 1535.0, 1.0), (30, 5, 1535.0, 1.0), (31, 0, 1.0, -64.0), (16, 6, 255.0, 1.0),
-                              (18, 6, -1.0, 1.0), (27, 11, 256.0, 0.0), (28, 5, 256.0, 0.0),
-                              (17, 6, 1.0, cf(33)), (19, 7, 1.0, cf(34)), (20, 7, 1.0, cf(35))):
-        lin(k, a, scale, bias)
-    for h in range(2):
-        act(B("tm", h, 128), A("VL", 0, 128), AF.Identity, bias=cf(25 + h), scale=cf(23 + h))
+    lin(15, 2, 16.0, 15.0)
+    lin(9, 2, 16.0, 1.0)
+    lin(10, 2, 16.0, 0.0)
+    lin(11, 5, 15.0, cf(10))
+    lin(17, 4, 2.0, cf(9))
+    for k, a in ((20, 6), (24, 5)):
+        lin(k, a, NV - 1.0 / 16, 1.0 / 16)
+        lin(k + 1, a, -31.0 * NV, 15.0 * NV)
+        lin(k + 2, a, 1.0 / 16 - 1.0 / (16 * NV), 1.0 / (16 * NV))
     act(Mx(mNI), Mx(mI), scale=-1.0)
     act(A("I32m", 0, 128), Mx(mI))
-    act(Mx(m256), Mx(mI), scale=256.0)
-    act(Mx(m8), Mx(mI), scale=-8.0)
-    act(Mx(m64k), Mx(mI), scale=65536.0)
+    act(Mx(mW1, 64), Mx(mWc, 64), scale=cf(20))
+    act(Mx(mW1, 64, 64), Mx(mWc, 64), scale=cf(21))
+    act(Mx(mW3, 64), Mx(mWc, 64), scale=cf(6))
     act(A("XO", 1024, 2048), A("XO", 0, 1024), scale=0.5)
-    for h in range(2):
-        ts(B("N2", h, 512), B("rot_i", h, 512), R256, OP.add, R256, OP.subtract)
-    for h in range(2):
-        tt(B("N2", 2 + h, 512), B("rot_i", h, 512), B("N2", h, 512), OP.subtract)
-    act(A("jb", 0, 1024), A("N2", 1024, 2048), AF.Identity, bias=EIGHTH, scale=0.125)
-    ts(Mx(mWc, 64), XI(64), cf(3), EQ)
-    ts(Mx(mL00), XI(128), cf(10), EQ, cf(11), OP.mult)
-    ts(Mx(mL01), XI(128), cf(12), EQ, cf(13), OP.mult)
-    ts(Mx(mL10), XI(128), cf(10), EQ, cf(5), OP.mult)
-    ts(Mx(mL11), XI(128), cf(12), EQ, cf(14), OP.mult)
     for k, w in enumerate((32.0, -16.0, 16.0)):
         ts(B("Wg", k, 8), XI(8), cf(2), EQ, w, OP.mult)
-    add("v", lambda: g.vector.memset(Mx(mOne)[0], 1.0), [], [Mx(mOne)])
+    fill(Mx(mOne), 1.0)
+    fill(Mx(mK), 1024.0)
+    ts(A("cf", 40, 48), A("ci", 8, 16), -2.0, OP.mult, cf(0), OP.add)
+    tt(A("PI", 8, 16), A("cf", 40, 48), XI(8), OP.add)
+    ts(A("PI", 0, 8), A("PI", 8, 16), 2.0, OP.mult, cf(11), OP.subtract)
+    fill(B("FILL", 1, 1024), 0.0)
+    for h in range(2):
+        ts(B("hu", h, 512), B("rot_i", h, 512), -127.5, OP.add, 1.0 / 256, OP.mult)
+        ts(B("N2", h, 512), B("hu", h, 512), 256.0, OP.mult)
+        tt(B("N2", 2 + h, 512), B("rot_i", h, 512), B("N2", h, 512), OP.subtract)
+    for d in range(2):
+        dma("s", (T.LD[d:128:2, :], ("LD", 1024 * d, 1024 * d + 1024)), B("N2", d, 1024), "ld0")
+    fill(B("FILL", 2, 1024), 0.0)
+    ts(cf(16), cf(4), 0.0, EQ)
+    ts(Z(0), XI(144), cf(15), EQ, cf(16), OP.mult)
     for b in range(16):
         mm(PS(128 * b, 128 * b + 128), A("N2", b, 2048, 16, reg=(0, 2048)), Mx(mPig), True, True)
     for bank in (0, 1, 2, 3):
@@ -268,130 +273,49 @@ def rank_program(g, core, T, topo):
             ev("av"[bank & 1], A("T2", b, 2048, 16, reg=(128 * b, 128 * b + 128)), PS(128 * b, 128 * b + 128))
     for i in range(16):
         mm(PS(2048 + 64 * i, 2112 + 64 * i), A("T2", 128 * i, 128 * i + 128, reg=(0, 2048)), Mx(mWc, 64), True, True)
-    for ch in range(2):
-        for h in range(2):
-            o = B("ps", 2 * ch + h, 512)
-            mm(o, Mx(mL00 + 2 * ch), B("N2", 2 + h, 512), True, False)
-            mm(o, Mx(mL01 + 2 * ch), B("N2", h, 512), False, True)
-    ts(A("cf", 41, 48), A("ci", 9, 16), -2.0, OP.mult, cf(0), OP.add)
-    ts(A("cf", 48, 56), XI(8), 2.0, OP.mult)
     ts(A("Wv", 0, 64), A("Wv", 0, 64), cf(15), OP.subtract, 15.0, OP.add)
-    tt(A("PI", 1, 8), A("cf", 41, 48), A("cf", 49, 56), OP.add)
-    ts(Mx(mWl), XI(128), cf(21), EQ, cf(22), OP.mult)
 
-    def first_offsets(h):
-        ts(B("o3", h, 512), B("ps", 4 + h, 512), -3.5, OP.add, 0.125, OP.mult)
-        ts(B("o4", h, 512), B("o3", h, 512), -0.5, OP.add, 0.5, OP.mult)
+    def offsets(h):
+        ts(B("o4", h, 512), B("ps", 4 + h, 512), -7.5, OP.add, 1.0 / 16, OP.mult)
 
-    first_offsets(0)
-    for ch in range(2):
-        act(B("VER", ch, 1024), B("ps", ch, 1024))
+    offsets(0)
+    fill(B("FILL", 3, 1024), 0.0)
+    act(A("Wv", 64, 128), A("Wv", 0, 64), AF.Identity, bias=15360.0)
+    act(A("Wv", 128, 192), A("Wv", 0, 64), AF.Identity, bias=1024.0)
+    for k, w in ((1, 24), (2, 25), (3, 5)):
+        act(Z(k), XI(144), AF.Identity, bias=cf(17), scale=-1.0)
+    ver = lambda u: B("VER", 8 - u, 2048)
 
-    def bound_weights(part):
-        if part == 0:
-            first_offsets(1)
-            tt(Mx(mDF), Mx(mI), Mx(mWl), OP.subtract)
-        elif part == 1:
-            ts(A("tm", 256, 384), A("XG", 0, 128), cf(2), EQ)
-            ts(A("CI", 0, 8), XI(8), cf(1), EQ, cf(23), OP.add)
-            ts(A("CI", 8, 16), A("XI", 8, 16), cf(1), EQ, cf(24), OP.add)
-            later.pop(0)()
-        elif part == 4:
-            for h in range(2):
-                tt(Mx(mGV0 + h), B("tm", h, 128), A("tm", 256, 384), OP.mult)
-        elif part == 2:
-            act(A("Wv", 64, 128), A("Wv", 0, 64), AF.Identity, bias=15360.0)
-            act(A("Wv", 128, 192), A("Wv", 0, 64), AF.Identity, bias=14336.0)
-        else:
-            for i in range(16):
-                act(B("WB", i, 128), Mx(mGV0 + i // 8), scale=col("CI", i))
+    def versions(t):
+        for u in range(7, t - 1, -1):
+            add("g", lambda u=u: g.indirect_dma_start(ver(u)[0], None, T.LD[:], IndirectOffsetOnAxis(ap=col("PI", 8 * t + u)[0], axis=0),
+                                                      bounds_check=127),
+                [col("PI", 8 * t + u), (None, ("LD", 0, 2048))], [ver(u)], kind="d", n=16)
+        if t:
+            dma("s", ver(0), A("OUT", 0, 16384, p=ROWS))
+        dma("s", B("VER", 0, 1024), B("VER", 3, 1024))
+        dma("s", B("VER", 1, 1024), B("VER", 2, 1024))
 
-    def versions(hs):
-        for h in hs:
-            dma("s", (T.LD[:, 1024 * h:1024 * h + 1024], ("LD", 1024 * h, 1024 * h + 1024)), B("VER", h, 1024))
-        if 1 in hs:
-            for u in range(1, 8):
-                o = B("VER", u, 2048)
-                add("g", lambda o=o, u=u: g.indirect_dma_start(o[0], None, T.LD[:], IndirectOffsetOnAxis(ap=col("PI", u)[0], axis=0),
-                                                               bounds_check=127),
-                    [col("PI", u), (None, ("LD", 0, 2048))], [o], kind="d", n=16)
-
-    versions([0, 1])
-
-    later = [lambda: ts(Mx(mWl, 64), XI(64), cf(31), EQ),
-             lambda: ts(A("Zw", 0, 144), XI(144), cf(15), EQ, cf(16), OP.mult),
-             lambda: ts(A("Z2", 0, 144), XI(144), cf(17), EQ),
-             lambda: ts(Mx(mC0), A("XH", 0, 128), cf(9), EQ, cf(27), OP.mult),
-             lambda: ts(Mx(mC1), A("XH", 0, 128), cf(9), EQ, cf(28), OP.mult),
-             lambda: ts(Mx(mT0), XI(128), cf(19), EQ, cf(18), OP.mult),
-             lambda: ts(Mx(mT1), XI(128), cf(20), EQ, cf(18), OP.mult)]
+    versions(0)
 
     slot = [3072, 3200, 3328, 3456, 3584, 3712, 2048, 2560]
-    st = {"tile": 0, "ab": 0, "nb": 1, "ag": 0}
-    abslot, gslot, bnd, pre, fin = {}, {}, {}, {}, []
-
-    def ab(ip):
-        if ip not in abslot:
-            abslot[ip] = st["ab"] % 3
-            st["ab"] += 1
-        return abslot[ip]
+    st = {"tile": 0, "bank": 0, "out": 0}
+    bank = {}
 
     def red(ip, two):
         c = slot[st["tile"]]
         st["tile"] += 1
-        s = ab(ip)
+        c0 = 2048 * ip
         mm(PS(c, c + 128), A("CT", 128 * ip, 128 * ip + 128, p=(0, 1)), A("M", 128 * mOne, 128 * mOne + 128, p=(0, 1)), True, False)
-        for name, c0, w in ([("DY", 2048 * ip, 1), ("AB", 2048 * s, 0)] if two else [("AB", 2048 * s, 2)]):
+        for name, w in ([("DY", 1), ("AB", 0)] if two else [("AB", 2)]):
             for b in range(16):
                 mm(PS(c + b, c + 128, 16, reg=(c, c + 128)), A(name, c0 + b, c0 + 2048, 16, reg=(c0, c0 + 2048)),
                    B("Wg", w, 8), False, name == "AB" and b == 15)
 
-    def bound(i, c=None):
-        if c is None:
-            c = st["nb"] & 1
-            st["nb"] += 1
-        for h in range(2):
-            mm(B("ps", 2 * c + h, 512), B("WB", i, 128), B("tA", 2 * (i // 8) + h, 512), True, True)
-        return B("ps", c, 1024)
+    tb = A("TB", 0, 65536)
 
-    def premade(i, q, c):
-        pre[i] = B("BP", len(pre), 1024)
-        ev(q, pre[i], bound(i, c))
-
-    def done1(i):
-        pass
-
-    def wrapped(ip):
-        fin.append(("w", ip // 4))
-        for b in range(16):
-            mm(PS(3072 + 128 * ip, 3200 + 128 * ip), A("Zw", 15 - b, 143 - b),
-               A("DY", 2048 * ip + b, 2048 * ip + 2048, 16, reg=(2048 * ip, 2048 * ip + 2048)), False,
-               fin.count(("w", ip // 4)) == 4 and b == 15)
-
-    def digits(i):
-        fin.append(("l", i // 8))
-        for h in range(2):
-            mm(B("ps", 4 + h, 512), A("Z2", 14 - 2 * (i & 7), 142 - 2 * (i & 7)), B("DY", 2 * i + h, 512), False,
-               fin.count(("l", i // 8)) == 8)
-
-    def first(i):
-        if i < 2:
-            for h in range(2):
-                mm(B("ps", 4 + h, 512), Mx(mC0 + i), B("n2N", h, 512), True, False)
-        else:
-            for h in range(2):
-                o, r = (B("ps", 6 + h, 512), B("n2W", h, 512)) if i == 2 else (B("ps", 4 + h, 512), B("n2N", h, 512))
-                mm(o, Mx(m256), r, True, False)
-                mm(o, Mx(m64k), r, False, False)
-
-    def done2(i):
-        for h in range(2):
-            mm(B("ps", 4 + h, 512), A("Zw", 15 - i, 143 - i), B("DY", 2 * i + h, 512), False, len(fin) == 15)
-        fin.append(i)
-
-    def steps(text, xt, rt, off, done):
+    def steps(text, xt):
         xw = A(xt, 0, 4096) if xt else None
-        rw = A(rt, 0, 8192) if rt else None
         for word in text.split():
             c, i = word[0], int(word[1:])
             if c == "A":
@@ -405,14 +329,14 @@ def rank_program(g, core, T, topo):
                     mm(o, Mx(mI), B("DY", 2 * i + h, 512), True, False)
                     mm(o, Mx(mNI), B("XO", h, 512), False, True)
             elif c == "P":
-                act(B("AB", 2 * ab(i // 2) + (i & 1), 1024), B("ps", i & 1, 1024), AF.Abs)
+                act(B("AB", i, 1024), B("ps", i & 1, 1024), AF.Abs)
             elif c == "T":
                 red(i, False)
             elif c == "R":
-                ts(B("AB", ab(i), 2048), B("DY", i, 2048), 0.0, OP.max)
+                ts(B("AB", i, 2048), B("DY", i, 2048), 0.0, OP.max)
                 red(i, True)
             elif c == "Q":
-                act(B("AB", ab(i), 2048), B("DY", i, 2048), AF.Abs)
+                act(B("AB", i, 2048), B("DY", i, 2048), AF.Abs)
                 red(i, False)
             elif c == "x" and i == 0:
                 cp(A("kf", 0, 256), PS(3072, 3328))
@@ -422,162 +346,125 @@ def rank_program(g, core, T, topo):
                 tt(A("kf", 256, 384), A("kf", 0, 128), PS(2048, 2176), OP.max)
                 tt(A("kf", 384, 512), A("kf", 256, 384), A("kf", 128, 256), OP.max)
                 tt(A("kf", 0, 128), A("kf", 384, 512), PS(2560, 2688), OP.max)
-            elif c == "a":
-                gslot[i] = B("AB", st["ag"] % 6, 1024)
-                st["ag"] += 1
-                act(gslot[i], G(rw, B(off, i, 64)))
-            elif c == "j" and i == 0:
-                for h in range(2):
-                    mm(B("ps", h, 512), Mx(mT0), B("VER", h, 512), True, False)
-                    mm(B("ps", h, 512), Mx(mT1), B("VER", 2 + h, 512), False, True)
-                act(A("jb", 0, 1024), PS(0, 1024), AF.Identity, bias=EIGHTH, scale=0.125)
-            elif c == "j" and i < 3:
-                for h in range(2):
-                    o = B("ps", 2 + h, 512)
-                    if i == 1:
-                        mm(o, Mx(mI), B("N2", 2 + h, 512), True, False)
-                    else:
-                        mm(o, Mx(mT0), B("VER", h, 512), True, False)
-                        mm(o, Mx(mT1), B("VER", 2 + h, 512), False, False)
-                for h in range(2):
-                    mm(B("ps", 2 + h, 512), Mx(m8), B("jb", h, 512), False, True)
-            elif c == "j":
-                act(A("tA", 0, 1024), PS(1024, 2048), AF.Identity, bias=cf(29), scale=cf(11))
-                act(A("tA", 1024, 2048), PS(1024, 2048), AF.Identity, bias=cf(30), scale=cf(5))
-                act(A("n2N", 0, 1024), PS(1024, 2048), AF.Square, bias=7.0 - 1536, scale=-1.0)
-            elif c == "y":
-                bound_weights(i)
+            elif c in "ag":
+                ev("a" if c == "a" else "v", B("OUT", i, 1024), G(tb, B("oq", i, 64)))
             elif c == "w":
-                wrapped(i)
-            elif c == "l":
-                digits(i)
-            elif c == "c":
-                first(i)
-            elif c == "b":
-                bnd[i] = bound(i)
-            elif c == "m":
-                tt(B("DY", i, 1024), gslot[i], bnd[i], OP.min)
-                done(i)
-            elif c == "n":
-                for h in range(2):
-                    for k in (i, i + 1):
-                        s, b = gslot[k][1][1] + 512 * h, bnd[k][1][1] + 512 * h
-                        tt(B("DY", 2 * k + h, 512), A("AB", s, s + 512), PS(b, b + 512), OP.min)
-                        mm(B("ps", 4 + h, 512), A("Zw", 15 - k, 143 - k), B("DY", 2 * k + h, 512), False, k > i)
-                    ev("a", B("sm", h, 512), B("ps", 4 + h, 512))
-                    dma("s", hbm(T.yr, 512 * h, 512 * h + 512), B("sm", h, 512))
-            elif c == "g":
-                tt(B("DY", i, 1024), G(rw, B(off, i, 64)), pre[i], OP.min)
-                done(i)
+                o = 2048 + 128 * i
+                for b in range(16):
+                    mm(PS(o, o + 128), Z(0, 15 - b, 128),
+                       A("OUT", 2048 * i + b, 2048 * i + 2048, 16, reg=(2048 * i, 2048 * i + 2048)), b == 0, b == 15)
+                dma("s", (T.LD[i:128:8, :], ("LD", 256 * i, 256 * i + 256)), B("OUT", i, 2048, p=ROWS), "ld1")
             elif c == "o":
-                ts(B("o3b", i, 512), B("ps", 6 + i, 512), -3.5, OP.add, 0.125, OP.mult)
-                ts(B("o4", i, 512), B("o3b", i, 512), -0.5, OP.add, 0.5, OP.mult)
-            elif c == "L":
-                act(B("VER", i, 1024), PS(2048, 3072))
-                versions([i])
+                offsets(i)
+
+    def last_pairs(text):
+        for word in text.split():
+            head = word.rstrip("0123456789-")
+            lo, hi = [64 * int(x) for x in word[len(head):].split("-")]
+            n = hi - lo
+            if head in ("v", "a"):
+                o = 2048 * (st["out"] % 6)
+                st["out"] += 1
+                ev(head, A("OUT", o, o + 16 * n), G(tb, A("oq", lo, hi)))
+                bank[lo] = 512 * (st["bank"] % 8)
+                st["bank"] += 1
+                for i in range(16):
+                    mm(PS(bank[lo], bank[lo] + n), Z(0, 15 - i, 128), A("OUT", o + i, o + 16 * n, 16, reg=(o, o + 16 * n)),
+                       i == 0, i == 15)
+            elif head == "y":
+                dma("s", hbm(T.yr, lo, hi), A("sm", lo, hi), "yout")
+            else:
+                ev(head[1], A("sm", lo, hi), PS(bank[lo], bank[lo] + n))
 
     sf = lambda k: B("sf", k, 64)
     si = lambda k: B("si", k, 64)
     su = lambda k: B("su", k, 64)
 
+    def columns(t):
+        if t == 0:
+            act(A("NB0", 0, 2048), A("T2", 0, 2048), AF.Identity, bias=FLOOR, scale=cf(22))
+            for i in range(16):
+                o = PS(64 * i, 64 * i + 64)
+                mm(o, A("T2", 128 * i, 128 * i + 128, reg=(0, 2048)), Mx(mW1, 64), True, False)
+                mm(o, B("NB0", i, 128), Mx(mW1, 64, 64), False, False)
+                mm(o, B("NB0", i, 128), Mx(mW3, 64), False, True)
+        else:
+            act(A("NB1", 0, 2048), ver(0), AF.Identity, bias=FLOOR, scale=cf(26))
+            for h in range(2):
+                for ch in range(2):
+                    mm(B("ps", h, 512), Z(1, 1 - ch, 128), B("VER", 32 + 2 * ch + h, 512), ch == 0, False)
+                    for k in (2, 3):
+                        mm(B("ps", h, 512), Z(k, 1 - ch, 128), B("NB1", 2 * ch + h, 512), False, ch == 1 and k == 3)
+
     def table(t):
         mm(PS(3072, 3200), A("kf", 0, 128), A("I32m", 0, 128), True, True)
-        if t == 0:
-            bound_weights(1)
+        columns(t)
         cp(sf(0), PS(3072, 3136))
         tt(si(0), sf(0), PS(3136, 3200), OP.max)
         ts(si(1), si(0), 1, AND)
-        ts(si(2), si(0), 15, AND)
         cp(A("sb", 0, 64), si(1))
-        mm(PS(3584, 3648), Mx(mOne), A("sb", 0, 64), True, True)
-        if t == 0:
-            bound_weights(4)
-            bound_weights(3)
+        mm(PS(3584, 3648), Mx(mK), A("sb", 0, 64), True, True)
+        ts(si(2), si(0), 15, AND)
+        ts(sf(1), si(2), 1024.0, OP.mult)
+        tt(sf(2), sf(1), A("Wv", 128, 192), OP.add)
         add("v", lambda: g.vector.tensor_reduce(cf(32)[0], PS(3584, 3648)[0], AxisListType.X, OP.add), [PS(3584, 3648)], [cf(32)])
-        ts(si(3), si(2), cf(32), OP.add, 2048.0, OP.mult)
-        ts(si(4), si(3), 15 * 2048, AND)
-        ts(sf(2), si(4), 15000.0, OP.is_gt, 17408.0, OP.mult)
-        tt(sf(6), A("Wv", 128, 192), si(4), OP.subtract)
-        ts(sf(3), si(4), 30000.0, OP.is_gt, 13312.0, OP.mult)
-        ts(sf(4), si(4), 15000.0, OP.is_gt, 15360.0, OP.mult)
-        tt(sf(8), A("Wv", 64, 128), si(4), OP.subtract)
-        tt(sf(7), sf(2), sf(6), OP.add)
-        ts(sf(5), si(4), 30000.0, OP.is_gt, 15360.0, OP.mult)
-        tt(sf(9), sf(4), sf(8), OP.add)
-        tt(sf(12), sf(7), sf(3), OP.add)
-        tt(sf(13), sf(9), sf(5), OP.add)
-        cp(su(1), sf(12))
-        cp(su(0), sf(13))
-        RT = "RT%d" % t
-        ver = A("VER", 0, 16384)
-        c0 = 2048 * rank
-        n = 1024 // PIECES
-        place = lambda h, ch: 512 * (2 * (h & 1) + ch) + n * (h >> 1)
-        for h in range(PIECES + 1):
+        ts(si(3), sf(2), cf(32), OP.add)
+        ts(si(4), sf(2), cf(32), OP.add, 2.0, OP.mult)
+        ts(si(5), si(3), 16383, AND)
+        ts(si(6), si(4), 2048, AND)
+        ts(su(1), si(5), 1024.0, OP.add)
+        tt(sf(3), si(5), si(6), OP.add)
+        cp(su(0), sf(3))
+        ST = "ST%d" % t
+        win = A("VER", 0, 18432)
+        for h in range(PIECES):
             for ch in range(2):
-                if h < PIECES:
-                    ev("va"[ch], B("AB", 2 * h + ch, n), G(ver, B("su", PIECES * ch + h, n // 16)))
-                    mm(PS(place(h, ch), place(h, ch) + n), Mx(mDF), B("AB", 2 * h + ch, n), True, True)
-            if h > 0:
-                for ch in range(2):
-                    k = c0 + 2 * n * (h - 1)
-                    ev("va"[ch], A(RT, k + ch, k + 2 * n, 2, reg=(k + n * ch, k + n * ch + n)),
-                       PS(place(h - 1, ch), place(h - 1, ch) + n))
-                out_piece(RT, 2048, PIECES, t, h - 1)
-        hand_on(RT, 2048, PIECES, t)
+                ev("va"[ch], B(ST, 2 * (PIECES * rank + h) + ch, NV), G(win, B("su", PIECES * ch + h, NV // 16)))
+            out_piece(ST, 2048, PIECES, t, h)
+        hand_on(ST, 2048, PIECES, t)
         st["tile"] = 0
-        abslot.clear()
 
-    def lists(lo, hi):
-        ts(sf(10), si(2), -1024.0, OP.mult)
-        ts(sf(11), si(2), hi, OP.is_gt, 1024.0, OP.mult)
-        ts(sf(1), si(2), lo, OP.is_lt, 1024.0, OP.mult)
-        tt(sf(14), sf(10), A("Wv", 64, 128), OP.add)
-        tt(sf(15), sf(11), A("Wv", 0, 64), OP.add)
+    def lay(t):
+        who = {"o": core, "s": sib, "p": peer, "d": diag}
+        order = [c + str(h) for c in "os" for h in range(PIECES)]
+        for h in range(PIECES + 1):
+            order += (["p%d" % h] if h < PIECES else []) + (["d%d" % (h - 1)] if h else [])
+        for w in order:
+            k = PIECES * T.rank_of(who[w[0]]) + int(w[1])
+            dma("s", B("TB", k, 16 * NV, p=ROWS), B("ST%d" % t, k, 2 * NV), "lay%d" % t)
+
+    def lists():
+        tt(sf(14), A("Wv", 64, 128), sf(1), OP.subtract)
+        ts(sf(11), si(2), 9.5, OP.is_gt, 1024.0, OP.mult)
         cp(su(2), sf(14))
-        tt(sf(0), sf(15), sf(1), OP.add)
-        cp(su(3), sf(0))
+        tt(sf(15), sf(11), A("Wv", 0, 64), OP.add)
+        cp(su(3), sf(15))
         act(A("Zh", 0, 1024), G(A("DY", 0, 16384), su(2)), AF.Identity, bias=-0.25, scale=0.5)
+        ts(A("oq", 0, 1024), PS(0, 1024), 192.0 * (NV - 1), OP.add)
 
     def newx(out):
         tt(A("sm", 0, 1024), G(A("XO", 0, 2048), su(3)), A("Zh", 0, 1024), OP.add)
         ts(out, A("sm", 0, 1024), R1, OP.add, R1, OP.subtract)
 
-    vports = lambda text: [int(w[1:]) for w in text.split() if w[0] == "g"]
-
-    steps(VOTE1, "XT0", None, None, None)
+    steps(VOTE1, "XT0")
     table(0)
-    vp = vports(MIDDLE)
-    for i in range(16):
-        mm(PS(2048 + 64 * i, 2112 + 64 * i), A("T2", 128 * i, 128 * i + 128, reg=(0, 2048)), Mx(mWl, 64), True, True)
-    act(A("jw", 0, 1024), PS(2048, 3072), AF.Identity, bias=EIGHTH, scale=0.125)
-    lists(-1.0, 9.5)
-    premade(vp[0], "v", 0)
-    premade(vp[1], "v", 1)
-    for h in range(2):
-        mm(B("ps", 6 + h, 512), Mx(m8), B("jw", h, 512), True, False)
-        for i in range(8 * h, 8 * h + 8):
-            mm(PS(3072 + 64 * i, 3136 + 64 * i), A("T2", 128 * i, 128 * i + 128, reg=(0, 2048)), Mx(mWl, 64), False, i % 8 == 7)
-    act(A("n2W", 0, 1024), PS(3072, 4096), AF.Square, bias=7.0 - 1536, scale=-1.0)
+    lists()
+    lay(0)
     newx(B("XT1", rank, 1024))
-    for k, i in enumerate(vp[2:]):
-        premade(i, GAP1[k], (2, 0, 1, 3)[k & 3])
-    while later:
-        later.pop(0)()
-    share_x("XT1", "ax1")
+    for k, w in ((1, 24), (2, 25), (3, 5)):
+        ts(Z(k), Z(k), 0.0, EQ, cf(w), OP.mult)
+    share_x("XT1", "ax1", [tb])
     dma("s", A("XO", 0, 1024), B("XT1", rank, 1024))
-    steps(MIDDLE, "XT1", "RT0", "o3", done1)
+    act(A("XO", 1024, 2048), B("XT1", rank, 1024), scale=0.5)
+    steps(PAIRS1, None)
+    versions(1)
+    steps(VOTE2, "XT1")
     table(1)
-    lists(2.0 * len([w for w in MIDDLE.split() if w[0] == "A"]) - 6.5, 9.5)
-    act(A("XO", 1024, 2048), A("XO", 0, 1024), scale=0.5)
-    pre.clear()
-    fin.clear()
-    vp = vports(LAST)
-    for k, i in enumerate(vp):
-        premade(i, "vvvaa"[k], k & 3)
+    lists()
+    lay(1)
     newx(A("X2", 0, 1024))
     dma("s", hbm(T.yx, 0, 1024), A("X2", 0, 1024))
-    steps(LAST, None, "RT1", "o3b", done2)
+    last_pairs(PAIRS2)
 
     emit(g, T, Q, ops)
 
@@ -636,9 +523,8 @@ def arrange(ops):
 
 def emit(g, T, Q, ops):
     depend(ops)
-    if WINDOW >= 0:
-        ops = arrange(ops)
-        depend(ops)
+    ops = arrange(ops)
+    depend(ops)
     issue(g, T, Q, ops)
 
 
@@ -680,6 +566,10 @@ def issue(g, T, Q, ops):
     known = {q: {} for q in Q}
     snap = {}
     need = set()
+    final = {}
+    for n, o in enumerate(ops):
+        if o["kind"] == "d":
+            final[o["sem"]] = (n, final.get(o["sem"], (0, 0))[1] + 16)
     for n, o in enumerate(ops):
         if o["kind"] == "x":
             snap[n] = {}
@@ -687,6 +577,9 @@ def issue(g, T, Q, ops):
         kn = known[o["q"]]
         best = {}
         for m in o["deps"]:
+            if ops[m]["kind"] == "d":
+                m = final[ops[m]["sem"]][0]
+                assert m < n
             key = ops[m]["q"] if ops[m]["kind"] == "c" else ("e", m)
             best[key] = max(best.get(key, -1), m)
         waits = []
@@ -718,8 +611,8 @@ def issue(g, T, Q, ops):
             total[o["sem"]] = o["n"]
         elif o["kind"] == "d":
             o["fn"]().then_inc(T.sem[o["sem"]], 16)
-            o["at"] = (o["sem"], 16)
-            total[o["sem"]] = 16
+            o["at"] = (o["sem"], final[o["sem"]][1])
+            total[o["sem"]] = o["at"][1]
         else:
             ins = o["fn"]()
             if n in need:

@@ -2,6 +2,8 @@ from concourse.bass import DstId, RemoteDMATransfer, IndirectOffsetOnAxis
 from concourse.mybir import AluOpType as OP, AxisListType, ActivationFunctionType as AF
 
 BF, F32, I32, U16 = "bfloat16", "float32", "int32", "uint16"
+PIECES = 4
+NV = 1024 // PIECES
 
 
 def _sb(n, d):
@@ -10,38 +12,47 @@ def _sb(n, d):
 
 SCRATCH = {
     "ps": ("psum", [128, 4096], F32),
-    "BIG": _sb(81920, BF), "XT1": _sb(4096, BF), "ST1": _sb(8192, BF),
-    "rot_i": _sb(1024, I32), "hu": _sb(1024, U16), "o4": _sb(1024, U16), "oq": _sb(1024, U16),
-    "sm": _sb(1024, F32), "Zh": _sb(1024, F32), "X2": _sb(1024, BF), "XO": _sb(2048, BF),
-    "kf": _sb(512, F32), "sf": _sb(1024, F32), "si": _sb(512, I32), "sb": _sb(64, BF), "su": _sb(256, U16),
+    "BIG": _sb(81920, BF), "XT1": _sb(4096, BF), "VER1": _sb(18432, BF),
+    "rot_i": _sb(1024, I32), "o4": _sb(1024, U16), "oq": _sb(1024, U16),
+    "sm": _sb(1024, F32), "XO1": _sb(2048, BF),
+    "kf": _sb(512, F32), "sf": _sb(1024, F32), "si": _sb(448, I32), "sb": _sb(64, BF), "su": _sb(256, U16),
     "ci": _sb(64, I32), "cf": _sb(64, F32), "XI": _sb(144, F32), "Wv": _sb(192, F32), "I32m": _sb(128, F32),
-    "M": _sb(8 * 128, BF), "Z": _sb(4 * 144, BF), "Wg": _sb(32, BF), "CT": _sb(1024, BF), "PI": _sb(16, I32),
-    "LD": ("dram", [128, 2048], BF),
+    "M": _sb(8 * 128, BF), "Z": _sb(7 * 144, BF), "Wg": _sb(32, BF), "CT": _sb(1024, BF), "PI": _sb(16, I32),
+    "LD": ("dram", [128, 2048], BF), "SD": ("dram", [8 * PIECES, 128, 2 * NV], BF),
 }
-PART = {"TB": 0, "XT0": 0, "N2": 4096, "T2": 6144, "NB0": 8192, "FILL": 10240, "AB": 14336, "DY": 30720, "VER": 47104,
-        "OUT": 65536, "ST0": 65536, "NB1": 79872}
+PART = {"TB": 0, "XT0": 0, "N2": 4096, "T2": 6144, "NB0": 8192, "XO0": 10240, "FILL": 12288, "AB": 14336, "DY": 30720, "VER0": 47104,
+        "OUT": 65536, "ST": 75776, "Zh": 77824, "X2": 78848, "NB1": 79872}
 NDMA = 64
 WINDOW, SLOPE, GATHER = 0.0, 0.0, 1.3
+TURN = "avaa"
 KEEP = ("g", "s", "v", "a")
-PIECES = 4
-NV = 1024 // PIECES
-SEMAPHORES = (["cv", "ca", "ct", "cg", "lay0", "lay1", "ld0", "ld1", "yout"] + ["d%d" % k for k in range(NDMA)]
-              + ["ax1"] + ["%s%d%d" % (s, t, h) for s in ("ap", "as", "af") for t in range(3) for h in range(4)])
+SEMAPHORES = (["cv", "ca", "ct", "cg", "lay0", "lay1", "ld0", "ld1", "yout", "av0"] + ["d%d" % k for k in range(NDMA)]
+              + ["%s%d%d" % (s, t, h) for s in ("ap", "as", "af") for t in range(3) for h in range(4)])
 mI, mNI, mPig, mWc, mOne, mK, mW1, mW3 = range(8)
+SUMS = (32768.0, -16384.0, 16384.0)
 R1 = 1.5 * 2.0 ** 23
 FLOOR = 192 - 0.49
 
-VOTE = "A1 S0 S1 R3 D4 P0 S2 P1 S3 T0 A2 D5 R5 P2 S4 P3 S5 T1 D6 Q4 D7 x0 P4 P5 T2 Q6 R7 x1"
-VOTE1 = "A0 D3 o1 " + VOTE
-PAIRS1 = "g0 a1 w0 g2 a3 w1 g4 a5 w2 g6 a7 w3 g8 a9 w4 g10 o0 a11 w5 g12 a13 w6 g14 a15 w7"
-VOTE2 = "A0 D3 o1 " + VOTE
-PAIRS2 = ("v0-2 a2-4 v4-6 a6-8 ev0-2 ea2-4 y0-4 v8-10 a10-12 ev4-6 ea6-8 y4-8 v12-13 a13-14 ev8-10 ea10-12 y8-12 "
-          "v14-15 a15-16 ev12-13 ea13-14 ev14-15 ea15-16 y12-16")
+VOTE = "A2 S0 S1 R1 D4 P0 S4 P1 S5 T0 R4 A3 D5 P4 S6 P5 S7 T2 R5 E14 P6 S14 P7 T3 D6 q12 x0 P14 t14 d15 r15 x1 q13 x2 x3"
+VOTE1 = "A0 D1 " + VOTE
+PAIRS1 = "g0004 a0408 w0 g0816 a1624 w1 w2 g2432 w3 a3240 w4 g4048 w5 o0 a4856 w6 g5659 a5964 w7"
+VOTE2 = "A0 D1 o1 " + VOTE
+PAIRS2 = ("v0-2 a2-4 v4-6 a6-8 ev0-2 ea2-4 y0-4 v8-10 a10-12 ev4-6 ea6-8 y4-8 v12-13 a13-14 v14-15 a15-16 "
+          "ev8-10 ea10-12 y8-12 ev12-13 ea13-14 ev14-15 ea15-16 y12-16")
 
 
 def rank_program(g, core, T, topo):
     rank = T.rank_of(core)
+    helper = lambda c: [k for o in T.cores if topo.chip(o) != topo.chip(c) for k in topo.cores_of(o)
+                        if topo.die(k) == topo.die(c) and k not in T.cores][0]
+    second = lambda c: [k for k in topo.cores_of(c) if topo.die(k) == topo.die(c) and k not in T.cores][1]
     if rank is None:
+        for c in T.cores:
+            if helper(c) == core:
+                relay(g, core, c, T, topo)
+            if second(c) == core:
+                copies(g, core, c, 1, T, topo)
+                g.wait_ge(T.sem["d0"], 2 * len(topo.engines(core, c)))
         return
     others = [c for c in T.cores if c != core]
     sib = [c for c in others if topo.chip(c) == topo.chip(core)][0]
@@ -97,13 +108,13 @@ def rank_program(g, core, T, topo):
         size = lambda x: x[1][3]
         lat = 90
         if kind == "x":
-            cost, lat = 0, {"p": 5000, "s": 3500, "f": 3000, "x": 9000}[sem[1]]
+            cost, lat = 0, {"p": 5000, "s": 3500, "f": 3000, "v": 9000}[sem[1]]
         elif kind == "r":
             cost, lat = 700, 3000
         elif kind == "d":
             cost, lat = (1700 if q == "g" else 60), 3000
         elif q == "t":
-            cost, lat = max(64, size(rd[1])) * (1.7 if rd[0][1][0] == "kf" else 0.42), 190
+            cost, lat = max(64, size(rd[1])) * (1.7 if rd[0][1][0] == "kf" else 0.5), 190
         elif q == "g":
             cost = 130 + 1.7 * size(wr[0])
         elif rd and len(rd[0]) == 3:
@@ -153,13 +164,17 @@ def rank_program(g, core, T, topo):
     def nbits(m):
         return bin(m).count("1")
 
-    def send(parts, after=()):
+    def landing(t, c, h):
+        k = slot_of(t, T.rank_of(c), h)
+        return (T.SD[k], ("SD", k, k + 1))
+
+    def send(parts, after=(), to=None):
         def fn(ls):
             trs = []
             for v, dst, m, s in parts:
                 rid, pid, _ = topo.addr(dst)
                 trs.append(RemoteDMATransfer(dst_ids=[DstId(rid=rid, pnc=pid)], dma_engine_mask=m,
-                                             remote_sem=T.sem[s], src=v[0], dst=v[0]))
+                                             remote_sem=T.sem[s], src=v[0], dst=(to or v)[0]))
             g.remote_dma_fused(trs, local_sem=ls)
         add("g", fn, [v for v, _, _, _ in parts] + list(after), [], kind="r", n=sum(nbits(m) for _, _, m, _ in parts))
 
@@ -172,17 +187,11 @@ def rank_program(g, core, T, topo):
         off = topo.mask(src, far)
         return off, topo.mask(src, near) & ~off
 
-    def halves(src):
-        far = [c for c in T.cores if topo.chip(c) != topo.chip(src)][0]
-        e = topo.engines(src, far)
-        return sum(1 << k for k in e[:len(e) // 2]), sum(1 << k for k in e[len(e) // 2:])
-
     def share_x(name, sem, after):
         mine = B(name, rank, 1024)
-        h0, h1 = halves(core)
-        send([(mine, peer, h0, sem), (mine, diag, h1, sem), (mine, sib, split(core)[1], sem)], after)
-        arrives([B(name, T.rank_of(c), 1024) for c in others], sem,
-                nbits(halves(peer)[0]) + nbits(halves(diag)[1]) + nbits(split(sib)[1]))
+        send([(mine, helper(core), split(core)[0], "ap" + sem), (mine, sib, split(core)[1], "as" + sem)], after)
+        for c, s in ((sib, "as"), (peer, "ap"), (diag, "af")):
+            arrives([B(name, T.rank_of(c), 1024)], s + sem, nbits(split(c)[1]))
 
     def out_piece(name, n, k, t, h):
         v = B(name, k * rank + h, n // k)
@@ -205,39 +214,36 @@ def rank_program(g, core, T, topo):
     dma("a", B("XT0", 2 * rank + 1, 512), hbm(T.x, 512, 1024))
     dma("s", A("rot_i", 0, 512), hbm(T.rot, 0, 512))
     dma("a", A("rot_i", 512, 1024), hbm(T.rot, 512, 1024))
-    dma("s", A("XO", 0, 1024), hbm(T.x, 0, 1024))
+    dma("s", A("XO0", 0, 1024), hbm(T.x, 0, 1024))
     iota(A("ci", 0, 1), [[0, 1]], 0, 1, False)
     iota(A("XI", 0, 144), [[1, 144]], 0, 0)
-    iota(A("CT", 0, 1024, p=(0, 32)), [[-2, 8], [-1, 2], [0, 64]], 15, 0)
+    iota(A("CT", 0, 512, p=(0, 32)), [[-1024, 8], [0, 64]], 15 * 1024, 0)
     out_piece("XT0", 1024, 2, 2, 0)
     out_piece("XT0", 1024, 2, 2, 1)
     iota(A("Wv", 0, 64), [[16, 64]], 0, 1)
+    iota(A("CT", 512, 1024, p=(0, 32)), [[-1024, 8], [0, 64]], 7 * 1024, 0)
     hand_on("XT0", 1024, 2, 2)
     p = col("ci", 0)
     ci = lambda j: col("ci", j)
     cf = lambda j: col("cf", j)
     AND, SHR, EQ = OP.bitwise_and, OP.logical_shift_right, OP.is_equal
     XI = lambda n: A("XI", 0, n)
-    fill(B("FILL", 0, 1024), 0.0)
+    fill(A("FILL", 0, 2048), 0.0)
     ts(ci(1), p, 15, AND)
     ts(ci(2), p, 4, SHR)
     ts(ci(3), p, 63, AND)
     ts(ci(4), p, 7, AND)
     ts(ci(5), p, 3, SHR, 1, AND)
     ts(ci(6), p, 6, SHR)
-    ts(ci(7), p, 0, AND)
-    for u in range(8):
-        ts(ci(8 + u), p, u, AND)
-    cp(A("cf", 0, 8), A("ci", 0, 8))
+    cp(A("cf", 0, 7), A("ci", 0, 7))
     ts(cf(8), cf(1), 8.0, OP.mult, cf(2), OP.add)
-    ts(Mx(mPig), XI(128), cf(8), EQ)
-    ts(Mx(mWc, 64), XI(64), cf(3), EQ)
-    ts(Mx(mI), XI(128), cf(0), EQ)
     lin = lambda k, a, scale, bias: act(cf(k), cf(a), AF.Identity, bias=bias, scale=scale)
     lin(15, 2, 16.0, 15.0)
+    ts(Mx(mWc, 64), XI(64), cf(3), EQ)
+    ts(Mx(mPig), XI(128), cf(8), EQ)
+    ts(Mx(mI), XI(128), cf(0), EQ)
+    ts(Z(3), XI(144), cf(15), EQ)
     lin(9, 2, 16.0, 1.0)
-    lin(10, 2, 16.0, 0.0)
-    lin(11, 5, 15.0, cf(10))
     lin(17, 4, 2.0, cf(9))
     for k, a in ((20, 6), (24, 5)):
         lin(k, a, NV - 1.0 / 16, 1.0 / 16)
@@ -245,60 +251,63 @@ def rank_program(g, core, T, topo):
         lin(k + 2, a, 1.0 / 16 - 1.0 / (16 * NV), 1.0 / (16 * NV))
     act(Mx(mNI), Mx(mI), scale=-1.0)
     act(A("I32m", 0, 128), Mx(mI))
+    for k, w in enumerate(SUMS):
+        act(Z(4 + k), Z(3), scale=w)
+        act(B("Wg", k, 8), A("Z", 144 * 3 + 15, 144 * 3 + 128, 16), scale=w)
+    for h in range(2):
+        ts(B("oq", h, 512), B("rot_i", h, 512), -127.5, OP.add, 1.0 / 256, OP.mult)
+    for h in range(2):
+        ts(B("ps", 6 + h, 512), B("oq", h, 512), 256.0, OP.mult)
+        act(B("N2", h, 512), B("ps", 6 + h, 512))
+    for h in range(2):
+        tt(B("N2", 2 + h, 512), B("rot_i", h, 512), B("ps", 6 + h, 512), OP.subtract)
+    for d in range(2):
+        for k in range(8):
+            dma("s", (T.LD[16 * k + 8 * d:16 * k + 8 * d + 8, :], ("LD", 8 * d + k, 8 * d + k + 1)),
+                B("N2", d, 1024, p=(16 * k, 16 * k + 16)), "ld0")
+    act(Mx(mOne), XI(128), AF.Identity, bias=1.0, scale=0.0)
+    act(Mx(mK), XI(128), AF.Identity, bias=1024.0, scale=0.0)
     act(Mx(mW1, 64), Mx(mWc, 64), scale=cf(20))
     act(Mx(mW1, 64, 64), Mx(mWc, 64), scale=cf(21))
     act(Mx(mW3, 64), Mx(mWc, 64), scale=cf(6))
-    act(A("XO", 1024, 2048), A("XO", 0, 1024), scale=0.5)
-    for k, w in enumerate((32.0, -16.0, 16.0)):
-        ts(B("Wg", k, 8), XI(8), cf(2), EQ, w, OP.mult)
-    fill(Mx(mOne), 1.0)
-    fill(Mx(mK), 1024.0)
-    ts(A("cf", 40, 48), A("ci", 8, 16), -2.0, OP.mult, cf(0), OP.add)
-    tt(A("PI", 8, 16), A("cf", 40, 48), XI(8), OP.add)
-    ts(A("PI", 0, 8), A("PI", 8, 16), 2.0, OP.mult, cf(11), OP.subtract)
-    fill(B("FILL", 1, 1024), 0.0)
-    for h in range(2):
-        ts(B("hu", h, 512), B("rot_i", h, 512), -127.5, OP.add, 1.0 / 256, OP.mult)
-        ts(B("N2", h, 512), B("hu", h, 512), 256.0, OP.mult)
-        tt(B("N2", 2 + h, 512), B("rot_i", h, 512), B("N2", h, 512), OP.subtract)
-    for d in range(2):
-        dma("s", (T.LD[d:128:2, :], ("LD", 1024 * d, 1024 * d + 1024)), B("N2", d, 1024), "ld0")
-    fill(B("FILL", 2, 1024), 0.0)
+    for k, w in ((1, 15360.0), (2, 1024.0), (0, 0.0)):
+        lin(30 + k, 2, -16.0, w)
+        act(B("Wv", k, 64), A("Wv", 0, 64), AF.Identity, bias=cf(30 + k))
+    for u in range(2, 7):
+        ts(ci(8 + u), p, u, AND)
     ts(cf(16), cf(4), 0.0, EQ)
-    ts(Z(0), XI(144), cf(15), EQ, cf(16), OP.mult)
-    for b in range(16):
-        mm(PS(128 * b, 128 * b + 128), A("N2", b, 2048, 16, reg=(0, 2048)), Mx(mPig), True, True)
-    for bank in (0, 1, 2, 3):
-        for b in range(4 * bank, 4 * bank + 4):
-            ev("av"[bank & 1], A("T2", b, 2048, 16, reg=(128 * b, 128 * b + 128)), PS(128 * b, 128 * b + 128))
-    for i in range(16):
-        mm(PS(2048 + 64 * i, 2112 + 64 * i), A("T2", 128 * i, 128 * i + 128, reg=(0, 2048)), Mx(mWc, 64), True, True)
-    ts(A("Wv", 0, 64), A("Wv", 0, 64), cf(15), OP.subtract, 15.0, OP.add)
+    ts(A("cf", 42, 47), A("ci", 10, 15), -2.0, OP.mult, cf(0), OP.add)
+    tt(A("PI", 2, 7), A("cf", 42, 47), A("XI", 2, 7), OP.add)
 
-    def offsets(h):
-        ts(B("o4", h, 512), B("ps", 4 + h, 512), -7.5, OP.add, 1.0 / 16, OP.mult)
+    def offsets(h, n=512):
+        ts(B("o4", h, n), PS(2048 + 512 * h, 2048 + 512 * h + n), -7.5, OP.add, 1.0 / 16, OP.mult)
 
-    offsets(0)
-    fill(B("FILL", 3, 1024), 0.0)
-    act(A("Wv", 64, 128), A("Wv", 0, 64), AF.Identity, bias=15360.0)
-    act(A("Wv", 128, 192), A("Wv", 0, 64), AF.Identity, bias=1024.0)
-    for k, w in ((1, 24), (2, 25), (3, 5)):
-        act(Z(k), XI(144), AF.Identity, bias=cf(17), scale=-1.0)
-    ver = lambda u: B("VER", 8 - u, 2048)
+    for q in range(4):
+        for b in range(16):
+            mm(PS(512 * q + b, 512 * q + 512, 16, reg=(512 * q, 512 * q + 512)), A("N2", b, 2048, 16, reg=(0, 2048)),
+               Mx(mPig, 32, 32 * q), True, True)
+        ev(TURN[q], B("T2", q, 512), B("ps", q, 512))
+        for i in range(4):
+            mm(PS(2048 + 512 * q + 64 * i, 2112 + 512 * q + 64 * i), B("T2", 4 * q + i, 128), Mx(mWc, 64), True, True)
+            ops[-1]["first"] = 1
+        if q:
+            offsets(q - 1, 256)
+    offsets(3, 256)
+    later = [lambda: act(Z(0), Z(3), scale=cf(16))] + [
+        lambda k=k: act(Z(k), XI(144), AF.Identity, bias=cf(17), scale=-1.0) for k in (1, 2, 3)]
+    ver = lambda u: B("VER0", 8 - u, 2048)
+    ld = (T.LD[:], ("LD", 0, 2048))
+    e = topo.engines(core, second(core))
+    send([(ld, c, sum(1 << k for k in e[j::2]), "av0") for j, c in enumerate((helper(peer), second(core)))],
+         to=(T.BIG[:, 0:2048],))
+    arrives([A("VER0", 0, 4096), A("VER0", 14336, 18432)], "av0", 4 * len(e))
+    for u in range(6, 1, -1):
+        add("g", lambda u=u: g.indirect_dma_start(ver(u)[0], None, T.LD[:], IndirectOffsetOnAxis(ap=col("PI", u)[0], axis=0),
+                                                  bounds_check=127),
+            [col("PI", u), ld], [ver(u)], kind="d", n=16)
 
-    def versions(t):
-        for u in range(7, t - 1, -1):
-            add("g", lambda u=u: g.indirect_dma_start(ver(u)[0], None, T.LD[:], IndirectOffsetOnAxis(ap=col("PI", 8 * t + u)[0], axis=0),
-                                                      bounds_check=127),
-                [col("PI", 8 * t + u), (None, ("LD", 0, 2048))], [ver(u)], kind="d", n=16)
-        if t:
-            dma("s", ver(0), A("OUT", 0, 16384, p=ROWS))
-        dma("s", B("VER", 0, 1024), B("VER", 3, 1024))
-        dma("s", B("VER", 1, 1024), B("VER", 2, 1024))
-
-    versions(0)
-
-    slot = [3072, 3200, 3328, 3456, 3584, 3712, 2048, 2560]
+    slot = [3072, 3200, 3328, 3456, 3584, 3712]
+    straight = {12: 2048, 13: 0, 14: 2112, 15: 2560}
     st = {"tile": 0, "bank": 0, "out": 0}
     bank = {}
 
@@ -312,22 +321,32 @@ def rank_program(g, core, T, topo):
                 mm(PS(c + b, c + 128, 16, reg=(c, c + 128)), A(name, c0 + b, c0 + 2048, 16, reg=(c0, c0 + 2048)),
                    B("Wg", w, 8), False, name == "AB" and b == 15)
 
+    def red1(i, two):
+        o, c0 = PS(straight[i], straight[i] + 64), 1024 * i
+        mm(o, A("M", 128 * mOne, 128 * mOne + 128, p=(0, 1)), A("CT", 64 * i, 64 * i + 64, p=(0, 1)), True, False)
+        for name, w in ([("DY", 5), ("AB", 4)] if two else [("AB", 6)]):
+            for b in range(16):
+                mm(o, Z(w, 15 - b, 128), A(name, c0 + b, c0 + 1024, 16, reg=(c0, c0 + 1024)), False, name == "AB" and b == 15)
+
     tb = A("TB", 0, 65536)
+    sf = lambda k: B("sf", k, 64)
+    si = lambda k: B("si", k, 64)
+    su = lambda k: B("su", k, 64)
 
     def steps(text, xt):
-        xw = A(xt, 0, 4096) if xt else None
+        xw, xo = (A(xt, 0, 4096), "XO" + xt[2]) if xt else (None, None)
         for word in text.split():
             c, i = word[0], int(word[1:])
             if c == "A":
                 act(B("DY", i, 2048), G(xw, B("o4", i, 128)))
             elif c == "D":
                 for k in (2 * i, 2 * i + 1):
-                    tt(B("DY", k, 1024), G(xw, B("o4", k, 64)), A("XO", 0, 1024), OP.subtract)
+                    tt(B("DY", k, 1024), G(xw, B("o4", k, 64)), A(xo, 0, 1024), OP.subtract)
             elif c == "S":
                 for h in range(2):
                     o = B("ps", 2 * (i & 1) + h, 512)
                     mm(o, Mx(mI), B("DY", 2 * i + h, 512), True, False)
-                    mm(o, Mx(mNI), B("XO", h, 512), False, True)
+                    mm(o, Mx(mNI), B(xo, h, 512), False, True)
             elif c == "P":
                 act(B("AB", i, 1024), B("ps", i & 1, 1024), AF.Abs)
             elif c == "T":
@@ -338,22 +357,44 @@ def rank_program(g, core, T, topo):
             elif c == "Q":
                 act(B("AB", i, 2048), B("DY", i, 2048), AF.Abs)
                 red(i, False)
+            elif c == "E":
+                act(B("DY", i, 1024), G(xw, B("o4", i, 64)))
+            elif c == "d":
+                tt(B("DY", i, 1024), G(xw, B("o4", i, 64)), A(xo, 0, 1024), OP.subtract)
+            elif c == "r":
+                ts(B("AB", i, 1024), B("DY", i, 1024), 0.0, OP.max)
+                red1(i, True)
+            elif c == "q":
+                act(B("AB", i, 1024), B("DY", i, 1024), AF.Abs)
+                red1(i, False)
+            elif c == "t":
+                red1(i, False)
             elif c == "x" and i == 0:
                 cp(A("kf", 0, 256), PS(3072, 3328))
                 tt(A("kf", 256, 512), A("kf", 0, 256), PS(3328, 3584), OP.max)
-            elif c == "x":
+            elif c == "x" and i == 1:
                 tt(A("kf", 0, 256), A("kf", 256, 512), PS(3584, 3840), OP.max)
-                tt(A("kf", 256, 384), A("kf", 0, 128), PS(2048, 2176), OP.max)
-                tt(A("kf", 384, 512), A("kf", 256, 384), A("kf", 128, 256), OP.max)
-                tt(A("kf", 0, 128), A("kf", 384, 512), PS(2560, 2688), OP.max)
+                tt(A("kf", 256, 384), A("kf", 0, 128), A("kf", 128, 256), OP.max)
+                mm(PS(3840, 3968), A("kf", 256, 384), A("I32m", 0, 128), True, True)
+            elif c == "x" and i == 2:
+                cp(sf(4), PS(straight[14], straight[14] + 64))
+                cp(sf(5), PS(straight[15], straight[15] + 64))
+                tt(sf(6), sf(4), PS(straight[12], straight[12] + 64), OP.max)
+            elif c == "x":
+                tt(sf(7), sf(5), PS(3904, 3968), OP.max)
+                tt(sf(8), sf(6), PS(3840, 3904), OP.max)
+                tt(sf(9), sf(7), PS(straight[13], straight[13] + 64), OP.max)
             elif c in "ag":
-                ev("a" if c == "a" else "v", B("OUT", i, 1024), G(tb, B("oq", i, 64)))
+                lo, hi = i // 100, i % 100
+                ev("a" if c == "a" else "v", A("OUT", 256 * lo, 256 * hi), G(tb, A("oq", 16 * lo, 16 * hi)))
             elif c == "w":
                 o = 2048 + 128 * i
                 for b in range(16):
                     mm(PS(o, o + 128), Z(0, 15 - b, 128),
                        A("OUT", 2048 * i + b, 2048 * i + 2048, 16, reg=(2048 * i, 2048 * i + 2048)), b == 0, b == 15)
-                dma("s", (T.LD[i:128:8, :], ("LD", 256 * i, 256 * i + 256)), B("OUT", i, 2048, p=ROWS), "ld1")
+                for u, lo, n, src in ([(u, 2048 * (8 - u), 2048, 0) for u in range(8)] + [(7, 0, 1024, 1024), (7, 1024, 1024, 0)]):
+                    dma("s", A("VER1", lo, lo + n, p=(i ^ u, 128, 8), reg=(lo + i, lo + i + 1)),
+                        A("OUT", 2048 * i + src, 2048 * i + src + n, p=ROWS), "ld1")
             elif c == "o":
                 offsets(i)
 
@@ -363,7 +404,7 @@ def rank_program(g, core, T, topo):
             lo, hi = [64 * int(x) for x in word[len(head):].split("-")]
             n = hi - lo
             if head in ("v", "a"):
-                o = 2048 * (st["out"] % 6)
+                o = 2048 * (st["out"] % 5)
                 st["out"] += 1
                 ev(head, A("OUT", o, o + 16 * n), G(tb, A("oq", lo, hi)))
                 bank[lo] = 512 * (st["bank"] % 8)
@@ -376,38 +417,31 @@ def rank_program(g, core, T, topo):
             else:
                 ev(head[1], A("sm", lo, hi), PS(bank[lo], bank[lo] + n))
 
-    sf = lambda k: B("sf", k, 64)
-    si = lambda k: B("si", k, 64)
-    su = lambda k: B("su", k, 64)
-
     def columns(t):
         if t == 0:
             act(A("NB0", 0, 2048), A("T2", 0, 2048), AF.Identity, bias=FLOOR, scale=cf(22))
             for i in range(16):
                 o = PS(64 * i, 64 * i + 64)
-                mm(o, A("T2", 128 * i, 128 * i + 128, reg=(0, 2048)), Mx(mW1, 64), True, False)
+                mm(o, B("T2", i, 128), Mx(mW1, 64) + (cf(32)[1],), True, False)
                 mm(o, B("NB0", i, 128), Mx(mW1, 64, 64), False, False)
                 mm(o, B("NB0", i, 128), Mx(mW3, 64), False, True)
         else:
-            act(A("NB1", 0, 2048), ver(0), AF.Identity, bias=FLOOR, scale=cf(26))
+            act(A("NB1", 0, 2048), B("VER1", 8, 2048), AF.Identity, bias=FLOOR, scale=cf(26))
             for h in range(2):
                 for ch in range(2):
-                    mm(B("ps", h, 512), Z(1, 1 - ch, 128), B("VER", 32 + 2 * ch + h, 512), ch == 0, False)
+                    mm(B("ps", h, 512), Z(1, 1 - ch, 128), A("VER1", 16384 + 1024 * ch + 512 * h, 16896 + 1024 * ch + 512 * h,
+                                                             reg=(16384, 18432)) + (cf(32)[1],), ch == 0, False)
                     for k in (2, 3):
                         mm(B("ps", h, 512), Z(k, 1 - ch, 128), B("NB1", 2 * ch + h, 512), False, ch == 1 and k == 3)
 
     def table(t):
-        mm(PS(3072, 3200), A("kf", 0, 128), A("I32m", 0, 128), True, True)
+        tt(A("sb", 0, 64), sf(8), sf(9), OP.is_gt)
+        mm(PS(3072, 3136), Mx(mK), A("sb", 0, 64), True, True)
+        tt(si(0), sf(8), sf(9), OP.max)
+        ts(si(2), si(0), 15 * 1024, AND)
+        add("v", lambda: g.vector.tensor_reduce(cf(32)[0], PS(3072, 3136)[0], AxisListType.X, OP.add), [PS(3072, 3136)], [cf(32)])
+        tt(sf(2), si(2), A("Wv", 128, 192), OP.add)
         columns(t)
-        cp(sf(0), PS(3072, 3136))
-        tt(si(0), sf(0), PS(3136, 3200), OP.max)
-        ts(si(1), si(0), 1, AND)
-        cp(A("sb", 0, 64), si(1))
-        mm(PS(3584, 3648), Mx(mK), A("sb", 0, 64), True, True)
-        ts(si(2), si(0), 15, AND)
-        ts(sf(1), si(2), 1024.0, OP.mult)
-        tt(sf(2), sf(1), A("Wv", 128, 192), OP.add)
-        add("v", lambda: g.vector.tensor_reduce(cf(32)[0], PS(3584, 3648)[0], AxisListType.X, OP.add), [PS(3584, 3648)], [cf(32)])
         ts(si(3), sf(2), cf(32), OP.add)
         ts(si(4), sf(2), cf(32), OP.add, 2.0, OP.mult)
         ts(si(5), si(3), 16383, AND)
@@ -415,58 +449,118 @@ def rank_program(g, core, T, topo):
         ts(su(1), si(5), 1024.0, OP.add)
         tt(sf(3), si(5), si(6), OP.add)
         cp(su(0), sf(3))
-        ST = "ST%d" % t
-        win = A("VER", 0, 18432)
+        ST = "ST"
+        win = A("VER%d" % t, 0, 18432)
         for h in range(PIECES):
             for ch in range(2):
-                ev("va"[ch], B(ST, 2 * (PIECES * rank + h) + ch, NV), G(win, B("su", PIECES * ch + h, NV // 16)))
-            out_piece(ST, 2048, PIECES, t, h)
-        hand_on(ST, 2048, PIECES, t)
+                ev("va"[ch], B(ST, 2 * h + ch, NV), G(win, B("su", PIECES * ch + h, NV // 16)))
+            send([(B(ST, h, 2 * NV), helper(core), split(core)[0], "ap%d%d" % (t, h)),
+                  (B(ST, h, 2 * NV), sib, split(core)[1], "as%d%d" % (t, h))], to=landing(t, core, h))
+        for h in range(PIECES):
+            for c, s in ((sib, "as"), (peer, "ap"), (diag, "af")):
+                arrives([landing(t, c, h)], "%s%d%d" % (s, t, h), nbits(split(c)[1]))
         st["tile"] = 0
 
     def lay(t):
         who = {"o": core, "s": sib, "p": peer, "d": diag}
         order = [c + str(h) for c in "os" for h in range(PIECES)]
-        for h in range(PIECES + 1):
-            order += (["p%d" % h] if h < PIECES else []) + (["d%d" % (h - 1)] if h else [])
+        order += [c + str(h) for h in range(PIECES) for c in "pd"]
+        if t == 0:
+            place = lambda w: PIECES * T.rank_of(who[w[0]]) + int(w[1])
+            late = [w for w in order if place(w) == PART["XO0"] // (16 * NV) and w[0] in "os"]
+            order = [w for w in order[:-2] if w not in late] + late + order[-2:]
         for w in order:
-            k = PIECES * T.rank_of(who[w[0]]) + int(w[1])
-            dma("s", B("TB", k, 16 * NV, p=ROWS), B("ST%d" % t, k, 2 * NV), "lay%d" % t)
+            c, h = who[w[0]], int(w[1])
+            src = B("ST", h, 2 * NV) + (landing(t, sib, 0)[1],) if c == core else landing(t, c, h)
+            dma("s" if w[0] in "op" else "a", B("TB", PIECES * T.rank_of(c) + h, 16 * NV, p=ROWS), src, "lay%d" % t)
 
     def lists():
-        tt(sf(14), A("Wv", 64, 128), sf(1), OP.subtract)
-        ts(sf(11), si(2), 9.5, OP.is_gt, 1024.0, OP.mult)
+        tt(sf(14), A("Wv", 64, 128), si(2), OP.subtract)
+        ts(sf(11), si(2), 7.5 * 1024, OP.is_lt, 1024.0, OP.mult)
         cp(su(2), sf(14))
+        ts(sf(12), si(2), 1024.0, EQ, -1024.0, OP.mult)
+        ts(si(1), si(2), 14 * 1024, AND)
         tt(sf(15), sf(11), A("Wv", 0, 64), OP.add)
+        ts(sf(10), si(1), 12.0 * 1024, EQ, 1024.0, OP.mult)
+        tt(sf(13), sf(15), sf(12), OP.add)
+        tt(sf(15), sf(13), sf(10), OP.add)
         cp(su(3), sf(15))
-        act(A("Zh", 0, 1024), G(A("DY", 0, 16384), su(2)), AF.Identity, bias=-0.25, scale=0.5)
-        ts(A("oq", 0, 1024), PS(0, 1024), 192.0 * (NV - 1), OP.add)
+        act(A("Zh", 0, 1024), G(A("DY", 0, 16384), su(2)))
 
-    def newx(out):
-        tt(A("sm", 0, 1024), G(A("XO", 0, 2048), su(3)), A("Zh", 0, 1024), OP.add)
-        ts(out, A("sm", 0, 1024), R1, OP.add, R1, OP.subtract)
+    def newx(xo, out):
+        ts(A(xo, 1024, 2048), A(xo, 0, 1024), 2.0, OP.mult)
+        ts(B("oq", 0, 512), PS(0, 512), 192.0 * (NV - 1), OP.add)
+        tt(A("sm", 0, 1024), G(A(xo, 0, 2048), su(3)), A("Zh", 0, 1024), OP.add)
+        ts(B("oq", 1, 512), PS(512, 1024), 192.0 * (NV - 1), OP.add)
+        ts(A("o4", 0, 1024), A("sm", 0, 1024), 0.5, OP.mult, -0.25, OP.add)
+        cp(out, A("o4", 0, 1024))
 
     steps(VOTE1, "XT0")
     table(0)
     lists()
+    newx("XO0", B("XT1", rank, 1024))
+    for f in later:
+        f()
     lay(0)
-    newx(B("XT1", rank, 1024))
     for k, w in ((1, 24), (2, 25), (3, 5)):
         ts(Z(k), Z(k), 0.0, EQ, cf(w), OP.mult)
-    share_x("XT1", "ax1", [tb])
-    dma("s", A("XO", 0, 1024), B("XT1", rank, 1024))
-    act(A("XO", 1024, 2048), B("XT1", rank, 1024), scale=0.5)
+    share_x("XT1", "22", [tb])
+    dma("s", A("XO1", 0, 1024), B("XT1", rank, 1024) + (tb[1],))
     steps(PAIRS1, None)
-    versions(1)
     steps(VOTE2, "XT1")
     table(1)
     lists()
+    newx("XO1", A("X2", 0, 1024))
     lay(1)
-    newx(A("X2", 0, 1024))
-    dma("s", hbm(T.yx, 0, 1024), A("X2", 0, 1024))
+    dma("s", hbm(T.yx, 0, 1024), A("X2", 0, 1024) + (tb[1],))
     last_pairs(PAIRS2)
 
     emit(g, T, Q, ops)
+
+
+def slot_of(t, r, h):
+    return PIECES * (4 * t + r) + h
+
+
+def relay(g, core, src, T, topo):
+    dsts = [c for c in T.cores if topo.chip(c) == topo.chip(core)]
+    e = topo.engines(core, dsts[0])
+    masks = [sum(1 << k for k in e[0::2]), sum(1 << k for k in e[1::2])]
+    r = T.rank_of(src)
+    table = lambda t: [(t, h, T.SD[slot_of(t, r, h)]) for h in range(PIECES)]
+    pieces = table(0) + [(2, 2, T.XT1[:, 1024 * r:1024 * r + 1024])] + table(1)
+    copies(g, core, [c for c in dsts if topo.die(c) == topo.die(core)][0], 7, T, topo)
+    for t, h, v in pieces:
+        g.wait_ge(T.sem["ap%d%d" % (t, h)], len(topo.engines(src, core)))
+        trs = []
+        for c, m in zip(dsts, masks):
+            rid, pid, _ = topo.addr(c)
+            s = "ap" if topo.die(c) == topo.die(core) else "af"
+            trs.append(RemoteDMATransfer(dst_ids=[DstId(rid=rid, pnc=pid)], dma_engine_mask=m,
+                                         remote_sem=T.sem["%s%d%d" % (s, t, h)], src=v, dst=v))
+        g.remote_dma_fused(trs, local_sem=T.sem["d0"])
+    g.wait_ge(T.sem["d0"], (len(pieces) + 2) * len(e))
+
+
+def copies(g, core, near, u, T, topo):
+    rid, pid, _ = topo.addr(near)
+    e = topo.engines(core, near)
+    mine = lambda k, p=slice(0, 128), lo=0, n=2048: T.BIG[p, 2048 * k + lo:2048 * k + lo + n]
+    there = lambda lo, n: T.BIG[:, PART["VER0"] + lo:PART["VER0"] + lo + n]
+    back = lambda s, d, m: RemoteDMATransfer(dst_ids=[DstId(rid=rid, pnc=pid)], dma_engine_mask=sum(1 << k for k in m),
+                                             remote_sem=T.sem["av0"], src=s, dst=d)
+    landed = len(topo.engines(near, core)) // 2
+    g.sync.wait_ge(T.sem["av0"], landed)
+    for c in range(u + 1):
+        g.sync.dma_start(mine(1, slice(c ^ u, 128, u + 1)), mine(0, slice(c, 128, u + 1))).then_inc(T.sem["ld0"], 16)
+    if u == 1:
+        g.wait_ge(T.sem["av0"], landed)
+        g.remote_dma_fused([back(mine(0), there(16384, 2048), e)], local_sem=T.sem["d0"])
+    g.wait_ge(T.sem["ld0"], 16 * (u + 1))
+    g.remote_dma_fused([back(mine(1), there(2048 * (8 - u), 2048), e)], local_sem=T.sem["d0"])
+    if u == 7:
+        g.remote_dma_fused([back(mine(1, lo=1024, n=1024), there(0, 1024), e[0::2]),
+                            back(mine(1, n=1024), there(1024, 1024), e[1::2])], local_sem=T.sem["d0"])
 
 
 def arrange(ops):
@@ -505,7 +599,7 @@ def arrange(ops):
                 continue
             f = free.get(q, 0.0) if q else 0.0
             t0 = min(max(f, ready[k]) for k in cs)
-            k = max((c for c in cs if max(f, ready[c]) <= t0 + WINDOW), key=lambda c: (level[c] - SLOPE * c, -c))
+            k = max((c for c in cs if max(f, ready[c]) <= t0 + WINDOW), key=lambda c: (ops[c].get("first", 0), level[c], -c))
             if best is None or t0 < best[0]:
                 best = (t0, max(f, ready[k]), k)
         _, t, k = best

from concourse.bass import DstId, RemoteDMATransfer, IndirectOffsetOnAxis
from concourse.mybir import AluOpType as OP, AxisListType, ActivationFunctionType as AF

BF, F32, I32, U16 = "bfloat16", "float32", "int32", "uint16"
PIECES = 4
NV = 1024 // PIECES


def _sb(n, d):
    return ("sbuf", [128, n], d)


SCRATCH = {
    "ps": ("psum", [128, 4096], F32),
    "BIG": _sb(81920, BF), "XT1": _sb(4096, BF), "VER1": _sb(18432, BF),
    "rot_i": _sb(1024, I32), "o4": _sb(1024, U16), "oq": _sb(1024, U16),
    "sm": _sb(1024, F32), "XO1": _sb(2048, BF),
    "kf": _sb(512, F32), "sf": _sb(1024, F32), "si": _sb(448, I32), "sb": _sb(64, BF), "su": _sb(256, U16),
    "ci": _sb(64, I32), "cf": _sb(64, F32), "XI": _sb(144, F32), "Wv": _sb(192, F32), "I32m": _sb(128, F32),
    "M": _sb(8 * 128, BF), "Z": _sb(7 * 144, BF), "Wg": _sb(32, BF), "CT": _sb(1024, BF), "PI": _sb(16, I32),
    "LD": ("dram", [128, 2048], BF), "SD": ("dram", [8 * PIECES, 128, 2 * NV], BF),
}
PART = {"TB": 0, "XT0": 0, "N2": 4096, "T2": 6144, "NB0": 8192, "XO0": 10240, "FILL": 12288, "AB": 14336, "DY": 30720, "VER0": 47104,
        "OUT": 65536, "ST": 75776, "Zh": 77824, "X2": 78848, "NB1": 79872}
NDMA = 64
WINDOW, SLOPE, GATHER = 0.0, 0.0, 1.3
TURN = "avaa"
KEEP = ("g", "s", "v", "a")
SEMAPHORES = (["cv", "ca", "ct", "cg", "lay0", "lay1", "ld0", "ld1", "yout", "av0"] + ["d%d" % k for k in range(NDMA)]
              + ["%s%d%d" % (s, t, h) for s in ("ap", "as", "af") for t in range(3) for h in range(4)])
mI, mNI, mPig, mWc, mOne, mK, mW1, mW3 = range(8)
SUMS = (32768.0, -16384.0, 16384.0)
R1 = 1.5 * 2.0 ** 23
FLOOR = 192 - 0.49

VOTE = "A2 S0 S1 R1 D4 P0 S4 P1 S5 T0 R4 A3 D5 P4 S6 P5 S7 T2 R5 E14 P6 S14 P7 T3 D6 q12 x0 P14 t14 d15 r15 x1 q13 x2 x3"
VOTE1 = "A0 D1 " + VOTE
PAIRS1 = "g0004 a0408 w0 g0816 a1624 w1 w2 g2432 w3 a3240 w4 g4048 w5 o0 a4856 w6 g5659 a5964 w7"
VOTE2 = "A0 D1 o1 " + VOTE
PAIRS2 = ("v0-2 a2-4 v4-6 a6-8 ev0-2 ea2-4 y0-4 v8-10 a10-12 ev4-6 ea6-8 y4-8 v12-13 a13-14 v14-15 a15-16 "
          "ev8-10 ea10-12 y8-12 ev12-13 ea13-14 ev14-15 ea15-16 y12-16")


def rank_program(g, core, T, topo):
    rank = T.rank_of(core)
    helper = lambda c: [k for o in T.cores if topo.chip(o) != topo.chip(c) for k in topo.cores_of(o)
                        if topo.die(k) == topo.die(c) and k not in T.cores][0]
    second = lambda c: [k for k in topo.cores_of(c) if topo.die(k) == topo.die(c) and k not in T.cores][1]
    if rank is None:
        for c in T.cores:
            if helper(c) == core:
                relay(g, core, c, T, topo)
            if second(c) == core:
                copies(g, core, c, 1, T, topo)
                g.wait_ge(T.sem["d0"], 2 * len(topo.engines(core, c)))
        return
    others = [c for c in T.cores if c != core]
    sib = [c for c in others if topo.chip(c) == topo.chip(core)][0]
    peer = [c for c in others if topo.chip(c) != topo.chip(core) and topo.die(c) == topo.die(core)][0]
    diag = [c for c in others if c != sib and c != peer][0]
    Q = {"v": g.vector, "a": g.scalar, "t": g.tensor, "g": g, "s": g.sync}
    ops = []
    ndma = [0]

    def A(name, lo, hi, step=1, p=None, reg=None):
        reg = reg if reg else (lo, hi)
        n = -(-(hi - lo) // step)
        if name in PART:
            o = PART[name]
            name, lo, hi, reg = "BIG", lo + o, hi + o, (reg[0] + o, reg[1] + o)
        t = T[name]
        ps = slice(0, 128) if p is None else slice(*p)
        ap = t[ps, lo:hi] if step == 1 else t[ps, lo:hi:step]
        return (ap, (name,) + reg + (n,))

    def B(name, k, n, p=None):
        return A(name, n * k, n * k + n, p=p)

    def Mx(k, n=128, o=0):
        return A("M", 128 * k + o, 128 * k + o + n)

    def Z(k, lo=0, n=144):
        return A("Z", 144 * k + lo, 144 * k + lo + n)

    def col(name, j):
        return A(name, j, j + 1)

    def G(win, off):
        return (win[0].indirect(off[0]), win[1], off[1])

    def regs(xs):
        out = []
        for x in xs:
            if isinstance(x, tuple):
                out.extend(r[:3] for r in x[1:])
        return out

    def val(x):
        return x[0] if isinstance(x, tuple) else x

    def short(*xs):
        return 0.5 if all(SCRATCH[x[1][0]][2] in (BF, U16) for x in xs) else 1.0

    def add(q, fn, rd, wr, kind="c", sem=None, n=1, rate=1.0):
        if kind in ("d", "r") and sem is None:
            sem = "d%d" % ndma[0]
            ndma[0] += 1
        size = lambda x: x[1][3]
        lat = 90
        if kind == "x":
            cost, lat = 0, {"p": 5000, "s": 3500, "f": 3000, "v": 9000}[sem[1]]
        elif kind == "r":
            cost, lat = 700, 3000
        elif kind == "d":
            cost, lat = (1700 if q == "g" else 60), 3000
        elif q == "t":
            cost, lat = max(64, size(rd[1])) * (1.7 if rd[0][1][0] == "kf" else 0.5), 190
        elif q == "g":
            cost = 130 + 1.7 * size(wr[0])
        elif rd and len(rd[0]) == 3:
            cost = 60 + GATHER * 16 * (rd[0][2][2] - rd[0][2][1])
        else:
            cost = 60 + 0.83 * max(64, size(wr[0]) * rate)
        ops.append({"q": q, "fn": fn, "rd": regs(rd), "wr": regs(wr), "kind": kind, "sem": sem, "n": n, "cost": cost, "lat": lat})

    def ts(out, in0, s1, o0, s2=None, o1=None):
        if o1 is None:
            add("v", lambda: g.vector.tensor_scalar(out[0], in0[0], val(s1), None, o0), [in0, s1], [out], rate=short(out, in0))
        else:
            add("v", lambda: g.vector.tensor_scalar(out[0], in0[0], val(s1), val(s2), o0, o1), [in0, s1, s2], [out],
                rate=short(out, in0))

    def tt(out, a, b, op):
        add("v", lambda: g.vector.tensor_tensor(out[0], a[0], b[0], op), [a, b], [out],
            rate=1.0 if "ps" in (a[1][0], b[1][0]) else 2.0)

    def cp(out, a):
        add("v", lambda: g.vector.tensor_copy(out[0], a[0]), [a], [out])

    def fill(out, c):
        add("v", lambda: g.vector.memset(out[0], c), [], [out], rate=short(out))

    def act(out, a, f=AF.Copy, bias=0.0, scale=1.0):
        add("a", lambda: g.scalar.activation(out[0], a[0], f, bias=val(bias), scale=val(scale)), [a, bias, scale], [out])

    def ev(q, out, a):
        if q == "a":
            act(out, a)
        else:
            cp(out, a)

    def mm(out, l, r, start, stop):
        add("t", lambda: g.tensor.matmul(out[0], l[0], r[0], start, stop), [l, r], [out])

    def iota(out, pat, base, cm, small=True):
        if small:
            add("g", lambda: g.iota(out[0], pat, base, cm, allow_small_or_imprecise_dtypes=True), [], [out])
        else:
            add("g", lambda: g.iota(out[0], pat, base, cm), [], [out])

    def dma(q, out, a, sem=None):
        add(q, lambda: Q[q].dma_start(out[0], a[0]), [a], [out], kind="d", n=16, sem=sem)

    def nbits(m):
        return bin(m).count("1")

    def landing(t, c, h):
        k = slot_of(t, T.rank_of(c), h)
        return (T.SD[k], ("SD", k, k + 1))

    def send(parts, after=(), to=None):
        def fn(ls):
            trs = []
            for v, dst, m, s in parts:
                rid, pid, _ = topo.addr(dst)
                trs.append(RemoteDMATransfer(dst_ids=[DstId(rid=rid, pnc=pid)], dma_engine_mask=m,
                                             remote_sem=T.sem[s], src=v[0], dst=(to or v)[0]))
            g.remote_dma_fused(trs, local_sem=ls)
        add("g", fn, [v for v, _, _, _ in parts] + list(after), [], kind="r", n=sum(nbits(m) for _, _, m, _ in parts))

    def arrives(views, sem, n):
        add(None, None, [], views, kind="x", sem=sem, n=n)

    def split(src):
        far = [c for c in T.cores if topo.chip(c) != topo.chip(src)][0]
        near = [c for c in T.cores if c != src and topo.chip(c) == topo.chip(src)][0]
        off = topo.mask(src, far)
        return off, topo.mask(src, near) & ~off

    def share_x(name, sem, after):
        mine = B(name, rank, 1024)
        send([(mine, helper(core), split(core)[0], "ap" + sem), (mine, sib, split(core)[1], "as" + sem)], after)
        for c, s in ((sib, "as"), (peer, "ap"), (diag, "af")):
            arrives([B(name, T.rank_of(c), 1024)], s + sem, nbits(split(c)[1]))

    def out_piece(name, n, k, t, h):
        v = B(name, k * rank + h, n // k)
        off, on = split(core)
        send([(v, peer, off, "ap%d%d" % (t, h)), (v, sib, on, "as%d%d" % (t, h))])

    def hand_on(name, n, k, t):
        for h in range(k):
            piece = lambda c: B(name, k * T.rank_of(c) + h, n // k)
            arrives([piece(peer)], "ap%d%d" % (t, h), nbits(split(peer)[0]))
            arrives([piece(sib)], "as%d%d" % (t, h), nbits(split(sib)[1]))
            send([(piece(peer), sib, topo.mask(core, sib), "af%d%d" % (t, h))])
            arrives([piece(diag)], "af%d%d" % (t, h), nbits(topo.mask(sib, core)))

    PS = lambda lo, hi, step=1, reg=None: A("ps", lo, hi, step, None, reg)
    hbm = lambda t, lo, hi: (t[:, lo:hi], (t.name + "_h", lo, hi))
    ROWS = (0, 128, 8)

    dma("s", B("XT0", 2 * rank, 512), hbm(T.x, 0, 512))
    dma("a", B("XT0", 2 * rank + 1, 512), hbm(T.x, 512, 1024))
    dma("s", A("rot_i", 0, 512), hbm(T.rot, 0, 512))
    dma("a", A("rot_i", 512, 1024), hbm(T.rot, 512, 1024))
    dma("s", A("XO0", 0, 1024), hbm(T.x, 0, 1024))
    iota(A("ci", 0, 1), [[0, 1]], 0, 1, False)
    iota(A("XI", 0, 144), [[1, 144]], 0, 0)
    iota(A("CT", 0, 512, p=(0, 32)), [[-1024, 8], [0, 64]], 15 * 1024, 0)
    out_piece("XT0", 1024, 2, 2, 0)
    out_piece("XT0", 1024, 2, 2, 1)
    iota(A("Wv", 0, 64), [[16, 64]], 0, 1)
    iota(A("CT", 512, 1024, p=(0, 32)), [[-1024, 8], [0, 64]], 7 * 1024, 0)
    hand_on("XT0", 1024, 2, 2)
    p = col("ci", 0)
    ci = lambda j: col("ci", j)
    cf = lambda j: col("cf", j)
    AND, SHR, EQ = OP.bitwise_and, OP.logical_shift_right, OP.is_equal
    XI = lambda n: A("XI", 0, n)
    fill(A("FILL", 0, 2048), 0.0)
    ts(ci(1), p, 15, AND)
    ts(ci(2), p, 4, SHR)
    ts(ci(3), p, 63, AND)
    ts(ci(4), p, 7, AND)
    ts(ci(5), p, 3, SHR, 1, AND)
    ts(ci(6), p, 6, SHR)
    cp(A("cf", 0, 7), A("ci", 0, 7))
    ts(cf(8), cf(1), 8.0, OP.mult, cf(2), OP.add)
    lin = lambda k, a, scale, bias: act(cf(k), cf(a), AF.Identity, bias=bias, scale=scale)
    lin(15, 2, 16.0, 15.0)
    ts(Mx(mWc, 64), XI(64), cf(3), EQ)
    ts(Mx(mPig), XI(128), cf(8), EQ)
    ts(Mx(mI), XI(128), cf(0), EQ)
    ts(Z(3), XI(144), cf(15), EQ)
    lin(9, 2, 16.0, 1.0)
    lin(17, 4, 2.0, cf(9))
    for k, a in ((20, 6), (24, 5)):
        lin(k, a, NV - 1.0 / 16, 1.0 / 16)
        lin(k + 1, a, -31.0 * NV, 15.0 * NV)
        lin(k + 2, a, 1.0 / 16 - 1.0 / (16 * NV), 1.0 / (16 * NV))
    act(Mx(mNI), Mx(mI), scale=-1.0)
    act(A("I32m", 0, 128), Mx(mI))
    for k, w in enumerate(SUMS):
        act(Z(4 + k), Z(3), scale=w)
        act(B("Wg", k, 8), A("Z", 144 * 3 + 15, 144 * 3 + 128, 16), scale=w)
    for h in range(2):
        ts(B("oq", h, 512), B("rot_i", h, 512), -127.5, OP.add, 1.0 / 256, OP.mult)
    for h in range(2):
        ts(B("ps", 6 + h, 512), B("oq", h, 512), 256.0, OP.mult)
        act(B("N2", h, 512), B("ps", 6 + h, 512))
    for h in range(2):
        tt(B("N2", 2 + h, 512), B("rot_i", h, 512), B("ps", 6 + h, 512), OP.subtract)
    for d in range(2):
        for k in range(8):
            dma("s", (T.LD[16 * k + 8 * d:16 * k + 8 * d + 8, :], ("LD", 8 * d + k, 8 * d + k + 1)),
                B("N2", d, 1024, p=(16 * k, 16 * k + 16)), "ld0")
    act(Mx(mOne), XI(128), AF.Identity, bias=1.0, scale=0.0)
    act(Mx(mK), XI(128), AF.Identity, bias=1024.0, scale=0.0)
    act(Mx(mW1, 64), Mx(mWc, 64), scale=cf(20))
    act(Mx(mW1, 64, 64), Mx(mWc, 64), scale=cf(21))
    act(Mx(mW3, 64), Mx(mWc, 64), scale=cf(6))
    for k, w in ((1, 15360.0), (2, 1024.0), (0, 0.0)):
        lin(30 + k, 2, -16.0, w)
        act(B("Wv", k, 64), A("Wv", 0, 64), AF.Identity, bias=cf(30 + k))
    for u in range(2, 7):
        ts(ci(8 + u), p, u, AND)
    ts(cf(16), cf(4), 0.0, EQ)
    ts(A("cf", 42, 47), A("ci", 10, 15), -2.0, OP.mult, cf(0), OP.add)
    tt(A("PI", 2, 7), A("cf", 42, 47), A("XI", 2, 7), OP.add)

    def offsets(h, n=512):
        ts(B("o4", h, n), PS(2048 + 512 * h, 2048 + 512 * h + n), -7.5, OP.add, 1.0 / 16, OP.mult)

    for q in range(4):
        for b in range(16):
            mm(PS(512 * q + b, 512 * q + 512, 16, reg=(512 * q, 512 * q + 512)), A("N2", b, 2048, 16, reg=(0, 2048)),
               Mx(mPig, 32, 32 * q), True, True)
        ev(TURN[q], B("T2", q, 512), B("ps", q, 512))
        for i in range(4):
            mm(PS(2048 + 512 * q + 64 * i, 2112 + 512 * q + 64 * i), B("T2", 4 * q + i, 128), Mx(mWc, 64), True, True)
            ops[-1]["first"] = 1
        if q:
            offsets(q - 1, 256)
    offsets(3, 256)
    later = [lambda: act(Z(0), Z(3), scale=cf(16))] + [
        lambda k=k: act(Z(k), XI(144), AF.Identity, bias=cf(17), scale=-1.0) for k in (1, 2, 3)]
    ver = lambda u: B("VER0", 8 - u, 2048)
    ld = (T.LD[:], ("LD", 0, 2048))
    e = topo.engines(core, second(core))
    send([(ld, c, sum(1 << k for k in e[j::2]), "av0") for j, c in enumerate((helper(peer), second(core)))],
         to=(T.BIG[:, 0:2048],))
    arrives([A("VER0", 0, 4096), A("VER0", 14336, 18432)], "av0", 4 * len(e))
    for u in range(6, 1, -1):
        add("g", lambda u=u: g.indirect_dma_start(ver(u)[0], None, T.LD[:], IndirectOffsetOnAxis(ap=col("PI", u)[0], axis=0),
                                                  bounds_check=127),
            [col("PI", u), ld], [ver(u)], kind="d", n=16)

    slot = [3072, 3200, 3328, 3456, 3584, 3712]
    straight = {12: 2048, 13: 0, 14: 2112, 15: 2560}
    st = {"tile": 0, "bank": 0, "out": 0}
    bank = {}

    def red(ip, two):
        c = slot[st["tile"]]
        st["tile"] += 1
        c0 = 2048 * ip
        mm(PS(c, c + 128), A("CT", 128 * ip, 128 * ip + 128, p=(0, 1)), A("M", 128 * mOne, 128 * mOne + 128, p=(0, 1)), True, False)
        for name, w in ([("DY", 1), ("AB", 0)] if two else [("AB", 2)]):
            for b in range(16):
                mm(PS(c + b, c + 128, 16, reg=(c, c + 128)), A(name, c0 + b, c0 + 2048, 16, reg=(c0, c0 + 2048)),
                   B("Wg", w, 8), False, name == "AB" and b == 15)

    def red1(i, two):
        o, c0 = PS(straight[i], straight[i] + 64), 1024 * i
        mm(o, A("M", 128 * mOne, 128 * mOne + 128, p=(0, 1)), A("CT", 64 * i, 64 * i + 64, p=(0, 1)), True, False)
        for name, w in ([("DY", 5), ("AB", 4)] if two else [("AB", 6)]):
            for b in range(16):
                mm(o, Z(w, 15 - b, 128), A(name, c0 + b, c0 + 1024, 16, reg=(c0, c0 + 1024)), False, name == "AB" and b == 15)

    tb = A("TB", 0, 65536)
    sf = lambda k: B("sf", k, 64)
    si = lambda k: B("si", k, 64)
    su = lambda k: B("su", k, 64)

    def steps(text, xt):
        xw, xo = (A(xt, 0, 4096), "XO" + xt[2]) if xt else (None, None)
        for word in text.split():
            c, i = word[0], int(word[1:])
            if c == "A":
                act(B("DY", i, 2048), G(xw, B("o4", i, 128)))
            elif c == "D":
                for k in (2 * i, 2 * i + 1):
                    tt(B("DY", k, 1024), G(xw, B("o4", k, 64)), A(xo, 0, 1024), OP.subtract)
            elif c == "S":
                for h in range(2):
                    o = B("ps", 2 * (i & 1) + h, 512)
                    mm(o, Mx(mI), B("DY", 2 * i + h, 512), True, False)
                    mm(o, Mx(mNI), B(xo, h, 512), False, True)
            elif c == "P":
                act(B("AB", i, 1024), B("ps", i & 1, 1024), AF.Abs)
            elif c == "T":
                red(i, False)
            elif c == "R":
                ts(B("AB", i, 2048), B("DY", i, 2048), 0.0, OP.max)
                red(i, True)
            elif c == "Q":
                act(B("AB", i, 2048), B("DY", i, 2048), AF.Abs)
                red(i, False)
            elif c == "E":
                act(B("DY", i, 1024), G(xw, B("o4", i, 64)))
            elif c == "d":
                tt(B("DY", i, 1024), G(xw, B("o4", i, 64)), A(xo, 0, 1024), OP.subtract)
            elif c == "r":
                ts(B("AB", i, 1024), B("DY", i, 1024), 0.0, OP.max)
                red1(i, True)
            elif c == "q":
                act(B("AB", i, 1024), B("DY", i, 1024), AF.Abs)
                red1(i, False)
            elif c == "t":
                red1(i, False)
            elif c == "x" and i == 0:
                cp(A("kf", 0, 256), PS(3072, 3328))
                tt(A("kf", 256, 512), A("kf", 0, 256), PS(3328, 3584), OP.max)
            elif c == "x" and i == 1:
                tt(A("kf", 0, 256), A("kf", 256, 512), PS(3584, 3840), OP.max)
                tt(A("kf", 256, 384), A("kf", 0, 128), A("kf", 128, 256), OP.max)
                mm(PS(3840, 3968), A("kf", 256, 384), A("I32m", 0, 128), True, True)
            elif c == "x" and i == 2:
                cp(sf(4), PS(straight[14], straight[14] + 64))
                cp(sf(5), PS(straight[15], straight[15] + 64))
                tt(sf(6), sf(4), PS(straight[12], straight[12] + 64), OP.max)
            elif c == "x":
                tt(sf(7), sf(5), PS(3904, 3968), OP.max)
                tt(sf(8), sf(6), PS(3840, 3904), OP.max)
                tt(sf(9), sf(7), PS(straight[13], straight[13] + 64), OP.max)
            elif c in "ag":
                lo, hi = i // 100, i % 100
                ev("a" if c == "a" else "v", A("OUT", 256 * lo, 256 * hi), G(tb, A("oq", 16 * lo, 16 * hi)))
            elif c == "w":
                o = 2048 + 128 * i
                for b in range(16):
                    mm(PS(o, o + 128), Z(0, 15 - b, 128),
                       A("OUT", 2048 * i + b, 2048 * i + 2048, 16, reg=(2048 * i, 2048 * i + 2048)), b == 0, b == 15)
                for u, lo, n, src in ([(u, 2048 * (8 - u), 2048, 0) for u in range(8)] + [(7, 0, 1024, 1024), (7, 1024, 1024, 0)]):
                    dma("s", A("VER1", lo, lo + n, p=(i ^ u, 128, 8), reg=(lo + i, lo + i + 1)),
                        A("OUT", 2048 * i + src, 2048 * i + src + n, p=ROWS), "ld1")
            elif c == "o":
                offsets(i)

    def last_pairs(text):
        for word in text.split():
            head = word.rstrip("0123456789-")
            lo, hi = [64 * int(x) for x in word[len(head):].split("-")]
            n = hi - lo
            if head in ("v", "a"):
                o = 2048 * (st["out"] % 5)
                st["out"] += 1
                ev(head, A("OUT", o, o + 16 * n), G(tb, A("oq", lo, hi)))
                bank[lo] = 512 * (st["bank"] % 8)
                st["bank"] += 1
                for i in range(16):
                    mm(PS(bank[lo], bank[lo] + n), Z(0, 15 - i, 128), A("OUT", o + i, o + 16 * n, 16, reg=(o, o + 16 * n)),
                       i == 0, i == 15)
            elif head == "y":
                dma("s", hbm(T.yr, lo, hi), A("sm", lo, hi), "yout")
            else:
                ev(head[1], A("sm", lo, hi), PS(bank[lo], bank[lo] + n))

    def columns(t):
        if t == 0:
            act(A("NB0", 0, 2048), A("T2", 0, 2048), AF.Identity, bias=FLOOR, scale=cf(22))
            for i in range(16):
                o = PS(64 * i, 64 * i + 64)
                mm(o, B("T2", i, 128), Mx(mW1, 64) + (cf(32)[1],), True, False)
                mm(o, B("NB0", i, 128), Mx(mW1, 64, 64), False, False)
                mm(o, B("NB0", i, 128), Mx(mW3, 64), False, True)
        else:
            act(A("NB1", 0, 2048), B("VER1", 8, 2048), AF.Identity, bias=FLOOR, scale=cf(26))
            for h in range(2):
                for ch in range(2):
                    mm(B("ps", h, 512), Z(1, 1 - ch, 128), A("VER1", 16384 + 1024 * ch + 512 * h, 16896 + 1024 * ch + 512 * h,
                                                             reg=(16384, 18432)) + (cf(32)[1],), ch == 0, False)
                    for k in (2, 3):
                        mm(B("ps", h, 512), Z(k, 1 - ch, 128), B("NB1", 2 * ch + h, 512), False, ch == 1 and k == 3)

    def table(t):
        tt(A("sb", 0, 64), sf(8), sf(9), OP.is_gt)
        mm(PS(3072, 3136), Mx(mK), A("sb", 0, 64), True, True)
        tt(si(0), sf(8), sf(9), OP.max)
        ts(si(2), si(0), 15 * 1024, AND)
        add("v", lambda: g.vector.tensor_reduce(cf(32)[0], PS(3072, 3136)[0], AxisListType.X, OP.add), [PS(3072, 3136)], [cf(32)])
        tt(sf(2), si(2), A("Wv", 128, 192), OP.add)
        columns(t)
        ts(si(3), sf(2), cf(32), OP.add)
        ts(si(4), sf(2), cf(32), OP.add, 2.0, OP.mult)
        ts(si(5), si(3), 16383, AND)
        ts(si(6), si(4), 2048, AND)
        ts(su(1), si(5), 1024.0, OP.add)
        tt(sf(3), si(5), si(6), OP.add)
        cp(su(0), sf(3))
        ST = "ST"
        win = A("VER%d" % t, 0, 18432)
        for h in range(PIECES):
            for ch in range(2):
                ev("va"[ch], B(ST, 2 * h + ch, NV), G(win, B("su", PIECES * ch + h, NV // 16)))
            send([(B(ST, h, 2 * NV), helper(core), split(core)[0], "ap%d%d" % (t, h)),
                  (B(ST, h, 2 * NV), sib, split(core)[1], "as%d%d" % (t, h))], to=landing(t, core, h))
        for h in range(PIECES):
            for c, s in ((sib, "as"), (peer, "ap"), (diag, "af")):
                arrives([landing(t, c, h)], "%s%d%d" % (s, t, h), nbits(split(c)[1]))
        st["tile"] = 0

    def lay(t):
        who = {"o": core, "s": sib, "p": peer, "d": diag}
        order = [c + str(h) for c in "os" for h in range(PIECES)]
        order += [c + str(h) for h in range(PIECES) for c in "pd"]
        if t == 0:
            place = lambda w: PIECES * T.rank_of(who[w[0]]) + int(w[1])
            late = [w for w in order if place(w) == PART["XO0"] // (16 * NV) and w[0] in "os"]
            order = [w for w in order[:-2] if w not in late] + late + order[-2:]
        for w in order:
            c, h = who[w[0]], int(w[1])
            src = B("ST", h, 2 * NV) + (landing(t, sib, 0)[1],) if c == core else landing(t, c, h)
            dma("s" if w[0] in "op" else "a", B("TB", PIECES * T.rank_of(c) + h, 16 * NV, p=ROWS), src, "lay%d" % t)

    def lists():
        tt(sf(14), A("Wv", 64, 128), si(2), OP.subtract)
        ts(sf(11), si(2), 7.5 * 1024, OP.is_lt, 1024.0, OP.mult)
        cp(su(2), sf(14))
        ts(sf(12), si(2), 1024.0, EQ, -1024.0, OP.mult)
        ts(si(1), si(2), 14 * 1024, AND)
        tt(sf(15), sf(11), A("Wv", 0, 64), OP.add)
        ts(sf(10), si(1), 12.0 * 1024, EQ, 1024.0, OP.mult)
        tt(sf(13), sf(15), sf(12), OP.add)
        tt(sf(15), sf(13), sf(10), OP.add)
        cp(su(3), sf(15))
        act(A("Zh", 0, 1024), G(A("DY", 0, 16384), su(2)))

    def newx(xo, out):
        ts(A(xo, 1024, 2048), A(xo, 0, 1024), 2.0, OP.mult)
        ts(B("oq", 0, 512), PS(0, 512), 192.0 * (NV - 1), OP.add)
        tt(A("sm", 0, 1024), G(A(xo, 0, 2048), su(3)), A("Zh", 0, 1024), OP.add)
        ts(B("oq", 1, 512), PS(512, 1024), 192.0 * (NV - 1), OP.add)
        ts(A("o4", 0, 1024), A("sm", 0, 1024), 0.5, OP.mult, -0.25, OP.add)
        cp(out, A("o4", 0, 1024))

    steps(VOTE1, "XT0")
    table(0)
    lists()
    newx("XO0", B("XT1", rank, 1024))
    for f in later:
        f()
    lay(0)
    for k, w in ((1, 24), (2, 25), (3, 5)):
        ts(Z(k), Z(k), 0.0, EQ, cf(w), OP.mult)
    share_x("XT1", "22", [tb])
    dma("s", A("XO1", 0, 1024), B("XT1", rank, 1024) + (tb[1],))
    steps(PAIRS1, None)
    steps(VOTE2, "XT1")
    table(1)
    lists()
    newx("XO1", A("X2", 0, 1024))
    lay(1)
    dma("s", hbm(T.yx, 0, 1024), A("X2", 0, 1024) + (tb[1],))
    last_pairs(PAIRS2)

    emit(g, T, Q, ops)


def slot_of(t, r, h):
    return PIECES * (4 * t + r) + h


def relay(g, core, src, T, topo):
    dsts = [c for c in T.cores if topo.chip(c) == topo.chip(core)]
    e = topo.engines(core, dsts[0])
    masks = [sum(1 << k for k in e[0::2]), sum(1 << k for k in e[1::2])]
    r = T.rank_of(src)
    table = lambda t: [(t, h, T.SD[slot_of(t, r, h)]) for h in range(PIECES)]
    pieces = table(0) + [(2, 2, T.XT1[:, 1024 * r:1024 * r + 1024])] + table(1)
    copies(g, core, [c for c in dsts if topo.die(c) == topo.die(core)][0], 7, T, topo)
    for t, h, v in pieces:
        g.wait_ge(T.sem["ap%d%d" % (t, h)], len(topo.engines(src, core)))
        trs = []
        for c, m in zip(dsts, masks):
            rid, pid, _ = topo.addr(c)
            s = "ap" if topo.die(c) == topo.die(core) else "af"
            trs.append(RemoteDMATransfer(dst_ids=[DstId(rid=rid, pnc=pid)], dma_engine_mask=m,
                                         remote_sem=T.sem["%s%d%d" % (s, t, h)], src=v, dst=v))
        g.remote_dma_fused(trs, local_sem=T.sem["d0"])
    g.wait_ge(T.sem["d0"], (len(pieces) + 2) * len(e))


def copies(g, core, near, u, T, topo):
    rid, pid, _ = topo.addr(near)
    e = topo.engines(core, near)
    mine = lambda k, p=slice(0, 128), lo=0, n=2048: T.BIG[p, 2048 * k + lo:2048 * k + lo + n]
    there = lambda lo, n: T.BIG[:, PART["VER0"] + lo:PART["VER0"] + lo + n]
    back = lambda s, d, m: RemoteDMATransfer(dst_ids=[DstId(rid=rid, pnc=pid)], dma_engine_mask=sum(1 << k for k in m),
                                             remote_sem=T.sem["av0"], src=s, dst=d)
    landed = len(topo.engines(near, core)) // 2
    g.sync.wait_ge(T.sem["av0"], landed)
    for c in range(u + 1):
        g.sync.dma_start(mine(1, slice(c ^ u, 128, u + 1)), mine(0, slice(c, 128, u + 1))).then_inc(T.sem["ld0"], 16)
    if u == 1:
        g.wait_ge(T.sem["av0"], landed)
        g.remote_dma_fused([back(mine(0), there(16384, 2048), e)], local_sem=T.sem["d0"])
    g.wait_ge(T.sem["ld0"], 16 * (u + 1))
    g.remote_dma_fused([back(mine(1), there(2048 * (8 - u), 2048), e)], local_sem=T.sem["d0"])
    if u == 7:
        g.remote_dma_fused([back(mine(1, lo=1024, n=1024), there(0, 1024), e[0::2]),
                            back(mine(1, n=1024), there(1024, 1024), e[1::2])], local_sem=T.sem["d0"])


def arrange(ops):
    n = len(ops)
    before = [set(o["deps"]) | o["chain"] for o in ops]
    last = {}
    for k, o in enumerate(ops):
        if o["q"] in KEEP or o["kind"] == "d":
            if o["q"] in last:
                before[k].add(last[o["q"]])
            last[o["q"]] = k
        if o["kind"] == "r":
            last["r"] = k
        if o["kind"] == "x":
            before[k].add(last["r"])
    after = [[] for _ in ops]
    for k in range(n):
        for m in before[k]:
            after[m].append(k)
    lag = lambda m, k: 0 if (ops[m]["q"] == ops[k]["q"] and m not in ops[k]["deps"]) else ops[m]["lat"]
    level = [0.0] * n
    for k in range(n - 1, -1, -1):
        level[k] = ops[k]["cost"] + max([lag(k, j) + level[j] for j in after[k]] + [ops[k]["lat"]])
    left = [len(b) for b in before]
    ready = [0.0] * n
    cand = {}
    free = {}
    for k in range(n):
        if not left[k]:
            cand.setdefault(ops[k]["q"], []).append(k)
    order = []
    while len(order) < n:
        best = None
        for q, cs in cand.items():
            if not cs:
                continue
            f = free.get(q, 0.0) if q else 0.0
            t0 = min(max(f, ready[k]) for k in cs)
            k = max((c for c in cs if max(f, ready[c]) <= t0 + WINDOW), key=lambda c: (ops[c].get("first", 0), level[c], -c))
            if best is None or t0 < best[0]:
                best = (t0, max(f, ready[k]), k)
        _, t, k = best
        q = ops[k]["q"]
        cand[q].remove(k)
        free[q] = t + ops[k]["cost"]
        order.append(ops[k])
        for j in after[k]:
            ready[j] = max(ready[j], t + ops[k]["cost"] + lag(k, j))
            left[j] -= 1
            if not left[j]:
                cand.setdefault(ops[j]["q"], []).append(j)
    return order


def emit(g, T, Q, ops):
    depend(ops)
    ops = arrange(ops)
    depend(ops)
    issue(g, T, Q, ops)


def depend(ops):
    acc = {}
    for n, o in enumerate(ops):
        deps = set()
        o["chain"] = set()
        mine = []
        for w, rs in ((False, o["rd"]), (True, o["wr"])):
            for name, lo, hi in rs:
                if name == "ps":
                    mine.append((name, lo // 512 * 512, -(-hi // 512) * 512, w, lo, hi))
                else:
                    mine.append((name, lo, hi, w, lo, hi))
        for name, lo, hi, w, l2, h2 in mine:
            for (m, lo1, hi1, w1, l1, h1) in acc.get(name, []):
                if lo1 >= hi or lo >= hi1:
                    continue
                q1 = ops[m]["q"]
                if name == "ps":
                    if q1 == o["q"] and (q1 == "t" or not (w or w1) or l1 >= h2 or l2 >= h1):
                        o["chain"].add(m)
                        continue
                elif not (w or w1):
                    continue
                deps.add(m)
        for name, lo, hi, w, l2, h2 in mine:
            lst = acc.setdefault(name, [])
            if w and name != "ps":
                lst[:] = [e for e in lst if not (lo <= e[1] and e[2] <= hi)]
            elif name == "ps":
                lst[:] = [e for e in lst if not (lo <= e[1] and e[2] <= hi and (ops[e[0]]["q"] != o["q"] or o["q"] == "t"))]
            lst.append((n, lo, hi, w, l2, h2))
        o["deps"] = deps


def issue(g, T, Q, ops):
    known = {q: {} for q in Q}
    snap = {}
    need = set()
    final = {}
    for n, o in enumerate(ops):
        if o["kind"] == "d":
            final[o["sem"]] = (n, final.get(o["sem"], (0, 0))[1] + 16)
    for n, o in enumerate(ops):
        if o["kind"] == "x":
            snap[n] = {}
            continue
        kn = known[o["q"]]
        best = {}
        for m in o["deps"]:
            if ops[m]["kind"] == "d":
                m = final[ops[m]["sem"]][0]
                assert m < n
            key = ops[m]["q"] if ops[m]["kind"] == "c" else ("e", m)
            best[key] = max(best.get(key, -1), m)
        waits = []
        for key, m in sorted(best.items(), key=lambda kv: -kv[1]):
            if kn.get(key, -1) >= m:
                continue
            waits.append(m)
            need.add(m)
            kn[key] = m
            for k2, m2 in snap[m].items():
                if kn.get(k2, -1) < m2:
                    kn[k2] = m2
        o["waits"] = waits
        snap[n] = dict(kn)
    cnt = {q: 0 for q in Q}
    total = {}
    for n, o in enumerate(ops):
        if o["kind"] == "x":
            o["at"] = (o["sem"], o["n"])
            total[o["sem"]] = o["n"]
            continue
        q = Q[o["q"]]
        for m in o["waits"]:
            s, v = ops[m]["at"]
            q.wait_ge(T.sem[s], v)
        if o["kind"] == "r":
            o["fn"](T.sem[o["sem"]])
            o["at"] = (o["sem"], o["n"])
            total[o["sem"]] = o["n"]
        elif o["kind"] == "d":
            o["fn"]().then_inc(T.sem[o["sem"]], 16)
            o["at"] = (o["sem"], final[o["sem"]][1])
            total[o["sem"]] = o["at"][1]
        else:
            ins = o["fn"]()
            if n in need:
                cnt[o["q"]] += 1
                s = "c" + o["q"]
                ins.then_inc(T.sem[s], 1)
                o["at"] = (s, cnt[o["q"]])
                total[s] = cnt[o["q"]]
    for s in sorted(total):
        g.wait_ge(T.sem[s], total[s])
